import numpy as np
import ml_dtypes


def mxq(x, axis, fmt="e4m3"):
    dtype, down = {"e4m3": (ml_dtypes.float8_e4m3fn, 7), "e5m2": (ml_dtypes.float8_e5m2, 14)}[fmt]
    v = np.moveaxis(np.asarray(x, np.float32).astype(ml_dtypes.bfloat16).astype(np.float64), axis, -1)
    blocks = v.reshape(v.shape[:-1] + (-1, 32))
    amax = np.abs(blocks).max(-1, keepdims=True)
    byte = np.maximum(np.where(amax > 0, np.frexp(amax)[1] - 1 + 127, 0) - down, 1)
    scale = np.exp2(byte - 127.0)
    codes = (blocks / scale).astype(np.float32).astype(dtype).astype(np.float64)
    return np.moveaxis((codes * scale).reshape(v.shape), -1, axis)


WIDE = False


def mx_kscale(k):
    if not WIDE:
        return np.ones(k)
    levels = np.array([10, -10, 5, -5, 0])
    if k % 512:
        return np.exp2(np.random.permutation(np.resize(levels, k // 32))).repeat(32)
    a = np.empty((k // 512, 16))
    for p in range(k // 512):
        a[p, :8] = np.random.permutation(np.resize(levels, 8))
        for g in range(8):
            far = levels[np.abs(levels - a[p, g]) >= 10]
            a[p, g + 8] = far[np.random.randint(len(far))]
    return np.exp2(a.ravel()).repeat(32)


def f64(x):
    return np.asarray(x).astype(np.float64)


def striped(idx):
    return np.tile(idx.reshape(-1, 16).T, (8, 1)).astype(np.uint16)


def unstriped(offs):
    return offs[:16].T.reshape(-1).astype(np.int64)


def striped8(idx):
    return np.concatenate([x.reshape(-1, 16).T for x in idx]).astype(np.uint16)


def runs(offs, k):
    lists = np.stack([offs[16 * r : 16 * r + 16].T.reshape(-1) for r in range(8)]).astype(np.int64)
    return lists[np.arange(k) % 512 // 64]


def pack_weight(w):
    k, n = w.shape
    w = f64(np.asarray(w, np.float32).astype(ml_dtypes.bfloat16)).reshape(k // 32, 32, n)
    amax = np.abs(w).max(1)
    byte = np.clip(np.where(amax > 0, np.frexp(amax)[1] - 1 + 127 - 7, 1), 1, 254)
    scaled = (w * np.exp2(127.0 - byte)[:, None, :]).reshape(k, n).astype(np.float32)
    words = np.ascontiguousarray(scaled.reshape(k // 512, 128, 4, n).transpose(0, 1, 3, 2)).astype(ml_dtypes.float8_e4m3fn).view(np.uint8)
    return words, np.ascontiguousarray(byte.astype(np.uint8).reshape(k // 512, 16, n))


def unpack_weight(words, scales):
    g, p, n, _ = words.shape
    vals = np.ascontiguousarray(words).view(ml_dtypes.float8_e4m3fn).astype(np.float64) * np.repeat(np.exp2(scales.astype(np.float64) - 127.0), 8, axis=1)[..., None]
    return vals.transpose(0, 1, 3, 2).reshape(g * 512, n)


E2M1 = np.array([0.0, 0.5, 1.0, 1.5, 2.0, 3.0, 4.0, 6.0, -0.0, -0.5, -1.0, -1.5, -2.0, -3.0, -4.0, -6.0])


def pack_fp4(w):
    k, n = w.shape
    w = f64(np.asarray(w, np.float32).astype(ml_dtypes.bfloat16)).reshape(k // 32, 32, n)
    amax = np.abs(w).max(1)
    mant, ex = np.frexp(amax / 6.0)
    byte = np.clip(np.where(amax > 0, np.where(mant > 0.5, ex, ex - 1) + 127, 1), 1, 254)
    scaled = (w * np.exp2(127.0 - byte)[:, None, :]).reshape(k, n).astype(np.float32)
    c = np.ascontiguousarray(scaled.reshape(k // 512, 128, 4, n).transpose(0, 1, 3, 2)).astype(ml_dtypes.float4_e2m1fn).view(np.uint8) & 0xF
    words = (c[..., 0::2] | (c[..., 1::2] << 4)).reshape(k // 512, 128, 2 * n)
    return np.ascontiguousarray(words), np.ascontiguousarray(byte.astype(np.uint8).reshape(k // 512, 16, n))


def unpack_fp4(words, scales):
    g, _, n = scales.shape
    words = np.ascontiguousarray(words).reshape(g, 128, n, 2)
    nib = np.empty((g, 128, n, 4), np.uint8)
    nib[..., 0::2] = words & 0xF
    nib[..., 1::2] = words >> 4
    vals = E2M1[nib] * np.repeat(np.exp2(scales.astype(np.float64) - 127.0), 8, axis=1)[..., None]
    return vals.transpose(0, 1, 3, 2).reshape(g * 512, n)


def silu(v):
    return v / (1.0 + np.exp(-np.maximum(v, -700.0)))

def planes(y):
    n, m = y.shape
    v = y.astype(np.float32).astype(ml_dtypes.bfloat16).astype(np.float64).reshape(n // 32, 32, m)
    top = np.abs(v).max(1)
    byte = np.clip(np.where(top > 0, np.frexp(top)[1] - 1 + 127 - 7, 1), 1, 254)
    codes = (v * np.exp2(127.0 - byte)[:, None, :]).reshape(n, m).astype(np.float32).astype(ml_dtypes.float8_e4m3fn).view(np.uint8)
    words = codes.reshape(n // 512, 128, 4, m).transpose(0, 1, 3, 2)
    return np.ascontiguousarray(words), np.ascontiguousarray(byte.astype(np.uint8).reshape(n // 512, 16, m))


K, T, S, N, G, H = 512, 2048, 512, 512, 2048, 512


def setup_inputs():
    n = np.random.standard_normal
    s = mx_kscale(K)[:, None]
    u = mx_kscale(H)
    packed_xT = pack_weight(n((K, T)) * s)
    packed_dT = pack_weight(n((K, G)) / s)
    packed_w1 = pack_fp4(n((H, N)) / np.sqrt(H) / u[:, None])
    return {
        "x_words": packed_xT[0],
        "x_scales": packed_xT[1],
        "d_words": packed_dT[0],
        "d_scales": packed_dT[1],
        "gn": (np.random.uniform(0.5, 1.5, (H, 1)) * u[:, None]).astype(np.float32),
        "w1_words": packed_w1[0],
        "w1_scales": packed_w1[1],
        "offs": striped(np.random.permutation(T)[:S]),
        "kidx": striped8(np.random.randint(0, G, (8, H))),
        "nb": striped8(np.stack([np.random.permutation(S) for _ in range(8)])),
    }


def reference(x_words, x_scales, d_words, d_scales, gn, w1_words, w1_scales, offs, kidx, nb):
    d_kidx = unpack_weight(d_words, d_scales)[np.arange(K)[:, None], runs(kidx, K)]
    xq = unpack_weight(x_words, x_scales)[:, unstriped(offs)]
    s = 0.0625 * (d_kidx.T @ xq)
    z = f64(gn) * (silu(s + 0.5 * (s[np.arange(H)[:, None], runs(nb, H)])))
    out_0 = unpack_fp4(w1_words, w1_scales).T @ mxq(z, 0, "e4m3")
    return (out_0,) + planes(out_0)

@@ -1,0 +1,228 @@
+from contextlib import ExitStack
+
+import concourse.mybir as mybir
+
+K, T, S, N, G, H = 512, 2048, 512, 512, 2048, 512
+FLOPS = 2 * K * H * S + 2 * H * N * S
+
+F32 = mybir.dt.float32
+BF16 = mybir.dt.bfloat16
+I32 = mybir.dt.int32
+U32 = mybir.dt.uint32
+U16 = mybir.dt.uint16
+U8 = mybir.dt.uint8
+FP8X4 = mybir.dt.float8_e4m3fn_x4
+FP4X4 = mybir.dt.float4_e2m1fn_x4
+ADD = mybir.AluOpType.add
+MULT = mybir.AluOpType.mult
+COPY = mybir.ActivationFunctionType.Copy
+SILU = mybir.ActivationFunctionType.Silu
+
+P = 128
+PACK = 4
+HALF = S // 2
+CHUNKS = [(0, 256), (256, 128), (384, 128)]
+
+
+def tile_picked_scoremix_silu_po_kernel(
+    tc, x_words, x_scales, d_words, d_scales, gn, w1_words, w1_scales, offs, kidx, nb, out_0, out_1, out_2
+):
+    nc = tc.nc
+    with ExitStack() as ctx:
+        lists = ctx.enter_context(tc.tile_pool(name="lists", bufs=1))
+        keep = ctx.enter_context(tc.tile_pool(name="keep", bufs=1))
+        reuse = ctx.enter_context(tc.tile_pool(name="reuse", bufs=1))
+        psum = ctx.enter_context(tc.psum_pool(name="psum", bufs=1))
+
+        kidx_sb = lists.tile([P, H // 16], U16, name="kidx_sb")
+        offs_sb = lists.tile([P, S // 16], U16, name="offs_sb")
+        nb_sb = lists.tile([P, S // 16], U16, name="nb_sb")
+
+        def sb(name, shape, dtype, tag=None):
+            return keep.tile(shape, dtype, name=name, tag=tag or name, align_bytes=64)
+
+        d_scale_table = sb("d_scale_table", [P, G], U8)
+        x_scale_table = sb("x_scale_table", [P, T], U8)
+        d_table = sb("d_table", [P, G], I32)
+        x_table = reuse.tile([P, T], I32, name="x_table", align_bytes=64, offset=0)
+        planes = sb("planes", [P, H + S], U8)
+        w_scale_rows = sb("w_scale_rows", [P, N], U8)
+        w_raw = sb("w_raw", [P, 2 * N], U8)
+        gn_sb = sb("gn_sb", [P, PACK], F32)
+        silu_bias = sb("silu_bias", [P, 1], F32)
+
+        nc.vector.memset(x_scale_table[:].bitcast(I32), 0)
+        nc.vector.memset(w_scale_rows[:].bitcast(I32), 0)
+        nc.vector.memset(planes[:].bitcast(I32), 0)
+
+        nc.sync.dma_start(kidx_sb[:], kidx)
+        nc.sync.dma_start(
+            d_scale_table[:].bitcast(I32), d_scales[0].bitcast(I32).unsqueeze(1).to_broadcast([16, 8, G // 4])
+        )
+        nc.sync.dma_start(offs_sb[:], offs)
+        nc.sync.dma_start(d_table[:], d_words[0].rearrange("p n t -> p (n t)").bitcast(I32))
+        nc.sync.dma_start(nb_sb[:], nb)
+        nc.sync.dma_start(x_table[:], x_words[0].rearrange("p n t -> p (n t)").bitcast(I32))
+        nc.scalar.dma_start(x_scale_table[:].bitcast(I32)[0:P:8, :], x_scales[0].bitcast(I32))
+        nc.gpsimd.dma_start(w_raw[:].bitcast(I32), w1_words[0].bitcast(I32))
+        for q in range(4):
+            nc.gpsimd.dma_start(
+                w_scale_rows[:].bitcast(I32)[32 * q : 32 * q + 4, :], w1_scales[0].bitcast(I32)[4 * q : 4 * q + 4, :]
+            )
+        nc.gpsimd.dma_start(gn_sb[:], gn.rearrange("(p t) o -> p (t o)", t=PACK))
+
+        d_scale_picked = sb("d_scale_picked", [P, H], U8)
+        x_scale_picked = sb("x_scale_picked", [P, S], U8)
+        spread = sb("spread", [P, H + S], U8)
+        nc.vector.tensor_copy(d_scale_picked[:], d_scale_table[:].indirect(kidx_sb[:]))
+        zero = sb("zero", [P, 1], F32, tag="d_scale_table")
+        nc.vector.memset(zero[:], 0.0)
+        nc.scalar.activation(silu_bias[:], zero[:], SILU)
+        nc.vector.tensor_copy(x_scale_picked[:], x_scale_table[:].indirect(offs_sb[:]))
+        nc.vector.tensor_copy(
+            spread[:, :H].rearrange("p (t m) -> p m t", t=PACK), d_scale_picked[:].rearrange("p (m t) -> p m t", t=PACK)
+        )
+        nc.vector.tensor_copy(spread[:, H:].bitcast(I32), x_scale_picked[:].bitcast(I32))
+        for a in range(4):
+            nc.scalar.dma_start(planes[:].bitcast(I32)[a:P:32, :], spread[:].bitcast(I32)[8 * a : P : 32, :])
+
+        d_picked = sb("d_picked", [P, H], I32, tag="x_scale_table")
+        d_dealt = sb("d_dealt", [P, H], I32)
+        nc.vector.tensor_copy(d_picked[:].bitcast(U32), d_table[:].bitcast(U32).indirect(kidx_sb[:]))
+        nc.vector.tensor_copy(
+            d_dealt[:].rearrange("p (t m) -> p m t", t=PACK), d_picked[:].rearrange("p (m t) -> p m t", t=PACK)
+        )
+        x_picked = [
+            sb("x_picked0", [P, HALF], I32, tag="x_scale_picked"),
+            sb("x_picked1", [P, HALF], I32, tag="d_scale_picked"),
+        ]
+        for h in range(2):
+            nc.vector.tensor_copy(
+                x_picked[h][:].bitcast(U32), x_table[:].bitcast(U32).indirect(offs_sb[:, h * 16 : (h + 1) * 16])
+            )
+
+        w_dealt = reuse.tile([P, 2 * N], U8, name="w_dealt", align_bytes=64, offset=0)
+        w_plane = reuse.tile([P, N], U8, name="w_plane", align_bytes=64, offset=2 * N)
+
+        window = [sb("window%d" % t, [P, S], F32) for t in range(PACK)]
+        own = [sb("own%d" % t, [P, S], F32) for t in range(PACK)]
+        banks = {}
+        for pair in range(0, PACK, 2):
+            for h, t in [(h, t) for h in range(2) for t in (pair, pair + 1)]:
+                banks[t, h] = psum.tile([P, HALF], F32, name="s%d%d" % (t, h), tag="bank%d" % (4 * h + t))
+                nc.tensor.matmul_mx(
+                    out=banks[t, h][:],
+                    lhsT=d_dealt[:, t * P : (t + 1) * P].bitcast(FP8X4),
+                    lhsT_scale=planes[:, t * P : (t + 1) * P],
+                    rhs=x_picked[h][:].bitcast(FP8X4),
+                    rhs_scale=planes[:, H + h * HALF : H + (h + 1) * HALF],
+                    start=True,
+                    stop=True,
+                )
+        for t in range(PACK):
+            for h in range(2):
+                cols = slice(h * HALF, (h + 1) * HALF)
+                nc.scalar.copy(window[t][:, cols], banks[t, h][:])
+        nc.vector.tensor_scalar(own[0][:, :HALF], window[0][:, :HALF], 2.0, None, MULT)
+        nc.vector.tensor_copy(
+            w_dealt[:].rearrange("p (t m b) -> p m t b", t=PACK, b=2),
+            w_raw[:].rearrange("p (m t b) -> p m t b", t=PACK, b=2),
+        )
+        nc.vector.tensor_copy(
+            w_plane[:].rearrange("p (t m) -> p m t", t=PACK), w_scale_rows[:].rearrange("p (m t) -> p m t", t=PACK)
+        )
+
+        y_codes = sb("y_codes", [P, S], I32)
+        y_scales = sb("y_scales", [P, S], U8)
+        out_rows = out_0.rearrange("(p t) n -> p t n", t=PACK)
+        out_words = out_1[0].rearrange("p n t -> p (n t)").bitcast(I32)
+        acted, z, y, y_bf = {}, {}, {}, {}
+
+        def mix(c, t, mixed):
+            lo, width = CHUNKS[c]
+            if t == 0:
+                acted[c] = sb("acted%d" % c, [P, PACK, width], F32)
+            nc.vector.tensor_tensor(
+                mixed, window[t][:].indirect(nb_sb[:, lo // 16 : (lo + width) // 16]), own[t][:, lo : lo + width], ADD
+            )
+            nc.scalar.activation(acted[c][:, t, :], mixed, SILU, bias=silu_bias[:], scale=0.03125)
+
+        def weigh(c):
+            width = CHUNKS[c][1]
+            z[c] = sb("z%d" % c, [P, width * PACK], BF16)
+            nc.vector.tensor_tensor(
+                z[c][:].rearrange("p (c i t) -> p c t i", i=4, t=PACK),
+                acted[c][:].rearrange("p t (c i) -> p c t i", i=4),
+                gn_sb[:].unsqueeze(1).unsqueeze(3).to_broadcast([P, width // 4, PACK, 4]),
+                MULT,
+            )
+
+        def second_product(c, first_bank):
+            lo, width = CHUNKS[c]
+            z_codes = sb("z_codes%d" % c, [P, width], I32)
+            z_scales = sb("z_scales%d" % c, [P, width], U8)
+            nc.vector.quantize_mx(out=z_codes[:].bitcast(FP8X4), scales=z_scales[:], in_=z[c][:])
+            y[c] = sb("y%d" % c, [P, PACK, width], F32)
+            per_bank = 512 // width
+            for n, t0 in enumerate(range(0, PACK, per_bank)):
+                acc = psum.tile([P, per_bank, width], F32, name="y%d%d" % (c, t0), tag="bank%d" % (first_bank + n))
+                for t in range(t0, t0 + per_bank):
+                    nc.tensor.matmul_mx(
+                        out=acc[:, t - t0, :],
+                        lhsT=w_dealt[:, 2 * t * P : 2 * (t + 1) * P].bitcast(FP4X4),
+                        lhsT_scale=w_plane[:, t * P : (t + 1) * P],
+                        rhs=z_codes[:].bitcast(FP8X4),
+                        rhs_scale=z_scales[:],
+                        start=True,
+                        stop=True,
+                    )
+                nc.scalar.copy(y[c][:, t0 : t0 + per_bank, :], acc[:])
+            nc.sync.dma_start(out_rows[:, :, lo : lo + width], y[c][:])
+
+        def round_result(c):
+            width = CHUNKS[c][1]
+            y_bf[c] = sb("y_bf%d" % c, [P, width * PACK], BF16)
+            nc.vector.tensor_copy(
+                y_bf[c][:].rearrange("p (c i t) -> p c t i", i=4, t=PACK), y[c][:].rearrange("p t (c i) -> p c t i", i=4)
+            )
+
+        def hand_on(c):
+            lo, width = CHUNKS[c]
+            cols = slice(lo, lo + width)
+            nc.vector.quantize_mx(out=y_codes[:, cols].bitcast(FP8X4), scales=y_scales[:, cols], in_=y_bf[c][:])
+            nc.sync.dma_start(out_words[:, cols], y_codes[:, cols])
+
+        first = sb("mixed_first", [P, 3, HALF], F32)
+        last0 = sb("mixed_last0", [P, HALF], F32, tag="held")
+        for t in range(PACK):
+            if t > 0:
+                nc.vector.tensor_scalar(own[t][:, :HALF], window[t][:, :HALF], 2.0, None, MULT)
+            mix(0, t, first[:, t, :] if t < 3 else last0[:])
+            nc.scalar.activation(own[t][:, HALF:], banks[t, 1][:], COPY, scale=2.0)
+        lead1 = sb("mixed_lead1", [P, 128], F32)
+        mix(1, 0, lead1[:])
+        weigh(0)
+        rest1 = sb("mixed_rest1", [P, 3, 128], F32, tag="held")
+        mix(1, 1, rest1[:, 0, :])
+        second_product(0, 0)
+        mix(1, 2, rest1[:, 1, :])
+        mix(1, 3, rest1[:, 2, :])
+        lead2 = sb("mixed_lead2", [P, 128], F32, tag="acted0")
+        mix(2, 0, lead2[:])
+        weigh(1)
+        rest2 = sb("mixed_rest2", [P, 3, 128], F32, tag="held")
+        mix(2, 1, rest2[:, 0, :])
+        mix(2, 2, rest2[:, 1, :])
+        mix(2, 3, rest2[:, 2, :])
+        second_product(1, 2)
+        weigh(2)
+        round_result(0)
+        second_product(2, 3)
+        hand_on(0)
+        round_result(1)
+        hand_on(1)
+        round_result(2)
+        hand_on(2)
+        for q in range(4):
+            queue = nc.sync if q % 2 == 0 else nc.scalar
+            queue.dma_start(out_2[0].bitcast(I32)[4 * q : 4 * q + 4, :], y_scales[:].bitcast(I32)[32 * q : 32 * q + 4, :])

@@ -51,20 +51,24 @@ def tile_picked_scoremix_silu_po_kernel(
         gn_sb = sb("gn_sb", [P, PACK], F32)
         silu_bias = sb("silu_bias", [P, 1], F32)
 
-        nc.vector.memset(x_scale_table[:].bitcast(I32), 0)
+        zero = sb("zero", [P, 1], F32)
+        nc.vector.memset(zero[:], 0.0)
+        nc.scalar.activation(silu_bias[:], zero[:], SILU)
         nc.vector.memset(w_scale_rows[:].bitcast(I32), 0)
         nc.vector.memset(planes[:].bitcast(I32), 0)
 
-        nc.sync.dma_start(kidx_sb[:], kidx)
         nc.sync.dma_start(
             d_scale_table[:].bitcast(I32), d_scales[0].bitcast(I32).unsqueeze(1).to_broadcast([16, 8, G // 4])
         )
+        nc.sync.dma_start(kidx_sb[:], kidx)
         nc.sync.dma_start(offs_sb[:], offs)
+        nc.sync.dma_start(
+            x_scale_table[:].bitcast(I32), x_scales[0].bitcast(I32).unsqueeze(1).to_broadcast([16, 8, T // 4])
+        )
         nc.sync.dma_start(d_table[:], d_words[0].rearrange("p n t -> p (n t)").bitcast(I32))
-        nc.sync.dma_start(nb_sb[:], nb)
         nc.sync.dma_start(x_table[:], x_words[0].rearrange("p n t -> p (n t)").bitcast(I32))
-        nc.scalar.dma_start(x_scale_table[:].bitcast(I32)[0:P:8, :], x_scales[0].bitcast(I32))
-        nc.gpsimd.dma_start(w_raw[:].bitcast(I32), w1_words[0].bitcast(I32))
+        nc.sync.dma_start(nb_sb[:], nb)
+        nc.sync.dma_start(w_raw[:].bitcast(I32), w1_words[0].bitcast(I32))
         for q in range(4):
             nc.gpsimd.dma_start(
                 w_scale_rows[:].bitcast(I32)[32 * q : 32 * q + 4, :], w1_scales[0].bitcast(I32)[4 * q : 4 * q + 4, :]
@@ -75,9 +79,6 @@ def tile_picked_scoremix_silu_po_kernel(
         x_scale_picked = sb("x_scale_picked", [P, S], U8)
         spread = sb("spread", [P, H + S], U8)
         nc.vector.tensor_copy(d_scale_picked[:], d_scale_table[:].indirect(kidx_sb[:]))
-        zero = sb("zero", [P, 1], F32, tag="d_scale_table")
-        nc.vector.memset(zero[:], 0.0)
-        nc.scalar.activation(silu_bias[:], zero[:], SILU)
         nc.vector.tensor_copy(x_scale_picked[:], x_scale_table[:].indirect(offs_sb[:]))
         nc.vector.tensor_copy(
             spread[:, :H].rearrange("p (t m) -> p m t", t=PACK), d_scale_picked[:].rearrange("p (m t) -> p m t", t=PACK)
@@ -163,7 +164,7 @@ def tile_picked_scoremix_silu_po_kernel(
             z_scales = sb("z_scales%d" % c, [P, width], U8)
             nc.vector.quantize_mx(out=z_codes[:].bitcast(FP8X4), scales=z_scales[:], in_=z[c][:])
             y[c] = sb("y%d" % c, [P, PACK, width], F32)
-            per_bank = 512 // width
+            per_bank = 2
             for n, t0 in enumerate(range(0, PACK, per_bank)):
                 acc = psum.tile([P, per_bank, width], F32, name="y%d%d" % (c, t0), tag="bank%d" % (first_bank + n))
                 for t in range(t0, t0 + per_bank):
@@ -198,6 +199,9 @@ def tile_picked_scoremix_silu_po_kernel(
             if t > 0:
                 nc.vector.tensor_scalar(own[t][:, :HALF], window[t][:, :HALF], 2.0, None, MULT)
             mix(0, t, first[:, t, :] if t < 3 else last0[:])
+            if t == 2:
+                nc.scalar.activation(own[0][:, HALF:], banks[0, 1][:], COPY, scale=2.0)
+        for t in range(1, PACK):
             nc.scalar.activation(own[t][:, HALF:], banks[t, 1][:], COPY, scale=2.0)
         lead1 = sb("mixed_lead1", [P, 128], F32)
         mix(1, 0, lead1[:])
@@ -217,7 +221,7 @@ def tile_picked_scoremix_silu_po_kernel(
         second_product(1, 2)
         weigh(2)
         round_result(0)
-        second_product(2, 3)
+        second_product(2, 4)
         hand_on(0)
         round_result(1)
         hand_on(1)

@@ -21,7 +21,7 @@ SILU = mybir.ActivationFunctionType.Silu
 P = 128
 PACK = 4
 HALF = S // 2
-CHUNKS = [(0, 256), (256, 128), (384, 128)]
+CHUNK = 128
 
 
 def tile_picked_scoremix_silu_po_kernel(
@@ -41,20 +41,14 @@ def tile_picked_scoremix_silu_po_kernel(
         def sb(name, shape, dtype, tag=None):
             return keep.tile(shape, dtype, name=name, tag=tag or name, align_bytes=64)
 
-        d_scale_table = sb("d_scale_table", [P, G], U8)
+        d_scale_table = reuse.tile([P, G], U8, name="d_scale_table", align_bytes=64, offset=4 * T)
         x_scale_table = sb("x_scale_table", [P, T], U8)
-        d_table = sb("d_table", [P, G], I32)
+        d_table = reuse.tile([P, G], I32, name="d_table", align_bytes=64, offset=4 * T + G)
         x_table = reuse.tile([P, T], I32, name="x_table", align_bytes=64, offset=0)
         planes = sb("planes", [P, H + S], U8)
-        w_scale_rows = sb("w_scale_rows", [P, N], U8)
-        w_raw = sb("w_raw", [P, 2 * N], U8)
-        gn_sb = sb("gn_sb", [P, PACK], F32)
         silu_bias = sb("silu_bias", [P, 1], F32)
 
-        zero = sb("zero", [P, 1], F32)
-        nc.vector.memset(zero[:], 0.0)
-        nc.scalar.activation(silu_bias[:], zero[:], SILU)
-        nc.vector.memset(w_scale_rows[:].bitcast(I32), 0)
+        nc.vector.memset(x_scale_table[:].bitcast(I32), 0)
         nc.vector.memset(planes[:].bitcast(I32), 0)
 
         nc.sync.dma_start(
@@ -62,26 +56,23 @@ def tile_picked_scoremix_silu_po_kernel(
         )
         nc.sync.dma_start(kidx_sb[:], kidx)
         nc.sync.dma_start(offs_sb[:], offs)
-        nc.sync.dma_start(
-            x_scale_table[:].bitcast(I32), x_scales[0].bitcast(I32).unsqueeze(1).to_broadcast([16, 8, T // 4])
-        )
+        nc.sync.dma_start(nb_sb[:], nb)
         nc.sync.dma_start(d_table[:], d_words[0].rearrange("p n t -> p (n t)").bitcast(I32))
         nc.sync.dma_start(x_table[:], x_words[0].rearrange("p n t -> p (n t)").bitcast(I32))
-        nc.sync.dma_start(nb_sb[:], nb)
-        nc.sync.dma_start(w_raw[:].bitcast(I32), w1_words[0].bitcast(I32))
-        for q in range(4):
-            nc.gpsimd.dma_start(
-                w_scale_rows[:].bitcast(I32)[32 * q : 32 * q + 4, :], w1_scales[0].bitcast(I32)[4 * q : 4 * q + 4, :]
-            )
-        nc.gpsimd.dma_start(gn_sb[:], gn.rearrange("(p t) o -> p (t o)", t=PACK))
+        nc.scalar.dma_start(x_scale_table[:].bitcast(I32)[0:P:8, :], x_scales[0].bitcast(I32))
 
         d_scale_picked = sb("d_scale_picked", [P, H], U8)
         x_scale_picked = sb("x_scale_picked", [P, S], U8)
         spread = sb("spread", [P, H + S], U8)
         nc.vector.tensor_copy(d_scale_picked[:], d_scale_table[:].indirect(kidx_sb[:]))
+        zero = reuse.tile([P, 1], F32, name="zero", align_bytes=64, offset=4 * T + 2 * N)
+        nc.vector.memset(zero[:], 0.0)
+        nc.scalar.activation(silu_bias[:], zero[:], SILU)
+        w_raw = reuse.tile([P, 2 * N], U8, name="w_raw", align_bytes=64, offset=4 * T)
+        nc.sync.dma_start(w_raw[:].bitcast(I32), w1_words[0].bitcast(I32))
         nc.vector.tensor_copy(x_scale_picked[:], x_scale_table[:].indirect(offs_sb[:]))
         nc.vector.tensor_copy(
-            spread[:, :H].rearrange("p (t m) -> p m t", t=PACK), d_scale_picked[:].rearrange("p (m t) -> p m t", t=PACK)
+            spread[:, :H].rearrange("p (t m) -> p t m", t=PACK), d_scale_picked[:].rearrange("p (m t) -> p t m", t=PACK)
         )
         nc.vector.tensor_copy(spread[:, H:].bitcast(I32), x_scale_picked[:].bitcast(I32))
         for a in range(4):
@@ -91,8 +82,17 @@ def tile_picked_scoremix_silu_po_kernel(
         d_dealt = sb("d_dealt", [P, H], I32)
         nc.vector.tensor_copy(d_picked[:].bitcast(U32), d_table[:].bitcast(U32).indirect(kidx_sb[:]))
         nc.vector.tensor_copy(
-            d_dealt[:].rearrange("p (t m) -> p m t", t=PACK), d_picked[:].rearrange("p (m t) -> p m t", t=PACK)
+            d_dealt[:].rearrange("p (t c i) -> p c t i", t=PACK, i=4),
+            d_picked[:].rearrange("p (c i t) -> p c t i", t=PACK, i=4),
         )
+        gn_sb = reuse.tile([P, PACK], F32, name="gn_sb", align_bytes=64, offset=4 * T + G)
+        w_scale_rows = reuse.tile([P, N], U8, name="w_scale_rows", align_bytes=64, offset=4 * T + G + 64)
+        nc.sync.dma_start(gn_sb[:], gn.rearrange("(p t) o -> p (t o)", t=PACK))
+        for q in range(4):
+            rows = w1_scales[0].bitcast(I32)[4 * q : 4 * q + 4, :]
+            nc.sync.dma_start(
+                w_scale_rows[:].bitcast(I32)[32 * q : 32 * (q + 1), :], rows.unsqueeze(0).to_broadcast([8, 4, N // 4])
+            )
         x_picked = [
             sb("x_picked0", [P, HALF], I32, tag="x_scale_picked"),
             sb("x_picked1", [P, HALF], I32, tag="d_scale_picked"),
@@ -102,74 +102,88 @@ def tile_picked_scoremix_silu_po_kernel(
                 x_picked[h][:].bitcast(U32), x_table[:].bitcast(U32).indirect(offs_sb[:, h * 16 : (h + 1) * 16])
             )
 
-        w_dealt = reuse.tile([P, 2 * N], U8, name="w_dealt", align_bytes=64, offset=0)
-        w_plane = reuse.tile([P, N], U8, name="w_plane", align_bytes=64, offset=2 * N)
-
         window = [sb("window%d" % t, [P, S], F32) for t in range(PACK)]
         own = [sb("own%d" % t, [P, S], F32) for t in range(PACK)]
         banks = {}
-        for pair in range(0, PACK, 2):
-            for h, t in [(h, t) for h in range(2) for t in (pair, pair + 1)]:
-                banks[t, h] = psum.tile([P, HALF], F32, name="s%d%d" % (t, h), tag="bank%d" % (4 * h + t))
-                nc.tensor.matmul_mx(
-                    out=banks[t, h][:],
-                    lhsT=d_dealt[:, t * P : (t + 1) * P].bitcast(FP8X4),
-                    lhsT_scale=planes[:, t * P : (t + 1) * P],
-                    rhs=x_picked[h][:].bitcast(FP8X4),
-                    rhs_scale=planes[:, H + h * HALF : H + (h + 1) * HALF],
-                    start=True,
-                    stop=True,
-                )
+        for t, h in [(0, 0), (1, 0), (0, 1), (1, 1), (2, 0), (2, 1), (3, 0), (3, 1)]:
+            banks[t, h] = psum.tile([P, HALF], F32, name="s%d%d" % (t, h), tag="bank%d" % (2 * t + h))
+            nc.tensor.matmul_mx(
+                out=banks[t, h][:],
+                lhsT=d_dealt[:, t * P : (t + 1) * P].bitcast(FP8X4),
+                lhsT_scale=planes[:, t * P : (t + 1) * P],
+                rhs=x_picked[h][:].bitcast(FP8X4),
+                rhs_scale=planes[:, H + h * HALF : H + (h + 1) * HALF],
+                start=True,
+                stop=True,
+            )
         for t in range(PACK):
             for h in range(2):
-                cols = slice(h * HALF, (h + 1) * HALF)
-                nc.scalar.copy(window[t][:, cols], banks[t, h][:])
-        nc.vector.tensor_scalar(own[0][:, :HALF], window[0][:, :HALF], 2.0, None, MULT)
+                nc.scalar.copy(window[t][:, h * HALF : (h + 1) * HALF], banks[t, h][:])
+
+        w_dealt = reuse.tile([P, 2 * N], U8, name="w_dealt", align_bytes=64, offset=0)
         nc.vector.tensor_copy(
-            w_dealt[:].rearrange("p (t m b) -> p m t b", t=PACK, b=2),
-            w_raw[:].rearrange("p (m t b) -> p m t b", t=PACK, b=2),
+            w_dealt[:].rearrange("p (t m b) -> p t m b", t=PACK, b=2),
+            w_raw[:].rearrange("p (m t b) -> p t m b", t=PACK, b=2),
         )
+
+        mixed = sb("mixed", [P, PACK, S], F32)
+        acted = sb("acted", [P, PACK, S], F32)
+        weighed = sb("weighed", [P, PACK, S], BF16)
+
+        def double(t, cols):
+            nc.vector.tensor_scalar(own[t][:, cols], window[t][:, cols], 2.0, None, MULT)
+
+        def activate(t, cols):
+            nc.scalar.activation(acted[:, t, cols], mixed[:, t, cols], SILU, bias=silu_bias[:], scale=0.03125)
+            nc.scalar.activation(weighed[:, t, cols], acted[:, t, cols], COPY, scale=gn_sb[:, t : t + 1])
+
+        for t in range(PACK):
+            if t > 0:
+                double(t, slice(0, S))
+            for h in range(2):
+                cols = slice(h * HALF, (h + 1) * HALF)
+                if t == 0:
+                    double(t, cols)
+                nc.vector.tensor_tensor(
+                    mixed[:, t, cols], window[t][:].indirect(nb_sb[:, 16 * h : 16 * (h + 1)]), own[t][:, cols], ADD
+                )
+                if t < PACK - 1:
+                    activate(t, cols)
+                else:
+                    for lo in range(h * HALF, (h + 1) * HALF, CHUNK):
+                        activate(t, slice(lo, lo + CHUNK))
+        w_plane = sb("w_plane", [P, N], U8, tag="own3")
         nc.vector.tensor_copy(
-            w_plane[:].rearrange("p (t m) -> p m t", t=PACK), w_scale_rows[:].rearrange("p (m t) -> p m t", t=PACK)
+            w_plane[:].rearrange("p (t m) -> p t m", t=PACK), w_scale_rows[:].rearrange("p (m t) -> p t m", t=PACK)
         )
 
         y_codes = sb("y_codes", [P, S], I32)
         y_scales = sb("y_scales", [P, S], U8)
         out_rows = out_0.rearrange("(p t) n -> p t n", t=PACK)
         out_words = out_1[0].rearrange("p n t -> p (n t)").bitcast(I32)
-        acted, z, y, y_bf = {}, {}, {}, {}
+        chunks = S // CHUNK
+        z, y, y_bf = {}, {}, {}
 
-        def mix(c, t, mixed):
-            lo, width = CHUNKS[c]
-            if t == 0:
-                acted[c] = sb("acted%d" % c, [P, PACK, width], F32)
-            nc.vector.tensor_tensor(
-                mixed, window[t][:].indirect(nb_sb[:, lo // 16 : (lo + width) // 16]), own[t][:, lo : lo + width], ADD
-            )
-            nc.scalar.activation(acted[c][:, t, :], mixed, SILU, bias=silu_bias[:], scale=0.03125)
-
-        def weigh(c):
-            width = CHUNKS[c][1]
-            z[c] = sb("z%d" % c, [P, width * PACK], BF16)
-            nc.vector.tensor_tensor(
-                z[c][:].rearrange("p (c i t) -> p c t i", i=4, t=PACK),
-                acted[c][:].rearrange("p t (c i) -> p c t i", i=4),
-                gn_sb[:].unsqueeze(1).unsqueeze(3).to_broadcast([P, width // 4, PACK, 4]),
-                MULT,
+        def interleave(dst, src):
+            nc.vector.tensor_copy(
+                dst.rearrange("p (c i t) -> p c t i", i=4, t=PACK), src.rearrange("p t (c i) -> p c t i", i=4)
             )
 
-        def second_product(c, first_bank):
-            lo, width = CHUNKS[c]
-            z_codes = sb("z_codes%d" % c, [P, width], I32)
-            z_scales = sb("z_scales%d" % c, [P, width], U8)
+        def weave(c):
+            z[c] = sb("z%d" % c, [P, CHUNK * PACK], BF16)
+            interleave(z[c][:], weighed[:, :, c * CHUNK : (c + 1) * CHUNK])
+
+        def second_product(c):
+            z_codes = sb("z_codes%d" % c, [P, CHUNK], I32)
+            z_scales = sb("z_scales%d" % c, [P, CHUNK], U8)
             nc.vector.quantize_mx(out=z_codes[:].bitcast(FP8X4), scales=z_scales[:], in_=z[c][:])
-            y[c] = sb("y%d" % c, [P, PACK, width], F32)
-            per_bank = 2
-            for n, t0 in enumerate(range(0, PACK, per_bank)):
-                acc = psum.tile([P, per_bank, width], F32, name="y%d%d" % (c, t0), tag="bank%d" % (first_bank + n))
-                for t in range(t0, t0 + per_bank):
+            y[c] = sb("y%d" % c, [P, PACK, CHUNK], F32)
+            for pair in range(2):
+                acc = psum.tile([P, 2, CHUNK], F32, name="y%d%d" % (c, pair), tag="bank%d" % (2 * c + pair))
+                for u in range(2):
+                    t = 2 * pair + u
                     nc.tensor.matmul_mx(
-                        out=acc[:, t - t0, :],
+                        out=acc[:, u, :],
                         lhsT=w_dealt[:, 2 * t * P : 2 * (t + 1) * P].bitcast(FP4X4),
                         lhsT_scale=w_plane[:, t * P : (t + 1) * P],
                         rhs=z_codes[:].bitcast(FP8X4),
@@ -177,56 +191,29 @@ def tile_picked_scoremix_silu_po_kernel(
                         start=True,
                         stop=True,
                     )
-                nc.scalar.copy(y[c][:, t0 : t0 + per_bank, :], acc[:])
-            nc.sync.dma_start(out_rows[:, :, lo : lo + width], y[c][:])
+                nc.scalar.copy(y[c][:, 2 * pair : 2 * pair + 2, :], acc[:])
+            nc.sync.dma_start(out_rows[:, :, c * CHUNK : (c + 1) * CHUNK], y[c][:])
 
         def round_result(c):
-            width = CHUNKS[c][1]
-            y_bf[c] = sb("y_bf%d" % c, [P, width * PACK], BF16)
-            nc.vector.tensor_copy(
-                y_bf[c][:].rearrange("p (c i t) -> p c t i", i=4, t=PACK), y[c][:].rearrange("p t (c i) -> p c t i", i=4)
-            )
+            y_bf[c] = sb("y_bf%d" % c, [P, CHUNK * PACK], BF16)
+            interleave(y_bf[c][:], y[c][:])
 
         def hand_on(c):
-            lo, width = CHUNKS[c]
-            cols = slice(lo, lo + width)
+            cols = slice(c * CHUNK, (c + 1) * CHUNK)
             nc.vector.quantize_mx(out=y_codes[:, cols].bitcast(FP8X4), scales=y_scales[:, cols], in_=y_bf[c][:])
-            nc.sync.dma_start(out_words[:, cols], y_codes[:, cols])
 
-        first = sb("mixed_first", [P, 3, HALF], F32)
-        last0 = sb("mixed_last0", [P, HALF], F32, tag="held")
-        for t in range(PACK):
-            if t > 0:
-                nc.vector.tensor_scalar(own[t][:, :HALF], window[t][:, :HALF], 2.0, None, MULT)
-            mix(0, t, first[:, t, :] if t < 3 else last0[:])
-            if t == 2:
-                nc.scalar.activation(own[0][:, HALF:], banks[0, 1][:], COPY, scale=2.0)
-        for t in range(1, PACK):
-            nc.scalar.activation(own[t][:, HALF:], banks[t, 1][:], COPY, scale=2.0)
-        lead1 = sb("mixed_lead1", [P, 128], F32)
-        mix(1, 0, lead1[:])
-        weigh(0)
-        rest1 = sb("mixed_rest1", [P, 3, 128], F32, tag="held")
-        mix(1, 1, rest1[:, 0, :])
-        second_product(0, 0)
-        mix(1, 2, rest1[:, 1, :])
-        mix(1, 3, rest1[:, 2, :])
-        lead2 = sb("mixed_lead2", [P, 128], F32, tag="acted0")
-        mix(2, 0, lead2[:])
-        weigh(1)
-        rest2 = sb("mixed_rest2", [P, 3, 128], F32, tag="held")
-        mix(2, 1, rest2[:, 0, :])
-        mix(2, 2, rest2[:, 1, :])
-        mix(2, 3, rest2[:, 2, :])
-        second_product(1, 2)
-        weigh(2)
-        round_result(0)
-        second_product(2, 4)
-        hand_on(0)
-        round_result(1)
-        hand_on(1)
-        round_result(2)
-        hand_on(2)
+        for c in range(chunks + 1):
+            if c < chunks:
+                weave(c)
+            if c > 0:
+                second_product(c - 1)
+        for c in range(chunks + 1):
+            if c < chunks:
+                round_result(c)
+            if c > 0:
+                hand_on(c - 1)
+        nc.sync.dma_start(out_words[:, : S - CHUNK], y_codes[:, : S - CHUNK])
+        nc.sync.dma_start(out_words[:, S - CHUNK :], y_codes[:, S - CHUNK :])
         for q in range(4):
             queue = nc.sync if q % 2 == 0 else nc.scalar
             queue.dma_start(out_2[0].bitcast(I32)[4 * q : 4 * q + 4, :], y_scales[:].bitcast(I32)[32 * q : 32 * q + 4, :])

@@ -116,62 +116,68 @@ def tile_picked_scoremix_silu_po_kernel(
                 start=True,
                 stop=True,
             )
+        for t, h in [(0, 0), (1, 0), (0, 1), (1, 1), (2, 0), (2, 1), (3, 0), (3, 1)]:
+            nc.scalar.copy(window[t][:, h * HALF : (h + 1) * HALF], banks[t, h][:])
         for t in range(PACK):
-            for h in range(2):
-                nc.scalar.copy(window[t][:, h * HALF : (h + 1) * HALF], banks[t, h][:])
+            nc.scalar.activation(own[t][:, HALF:], banks[t, 1][:], COPY, scale=2.0)
 
         w_dealt = reuse.tile([P, 2 * N], U8, name="w_dealt", align_bytes=64, offset=0)
+        w_plane = reuse.tile([P, N], U8, name="w_plane", align_bytes=64, offset=2 * N)
+        halves = [sb("mixed%d" % h, [P, PACK, HALF], F32) for h in range(2)]
+
+        def double(t):
+            nc.vector.tensor_scalar(own[t][:, :HALF], window[t][:, :HALF], 2.0, None, MULT)
+
+        def mix(t, h):
+            nc.vector.tensor_tensor(
+                halves[h][:, t, :],
+                window[t][:].indirect(nb_sb[:, 16 * h : 16 * (h + 1)]),
+                own[t][:, h * HALF : (h + 1) * HALF],
+                ADD,
+            )
+
         nc.vector.tensor_copy(
             w_dealt[:].rearrange("p (t m b) -> p t m b", t=PACK, b=2),
             w_raw[:].rearrange("p (m t b) -> p t m b", t=PACK, b=2),
         )
-
-        mixed = sb("mixed", [P, PACK, S], F32)
-        acted = sb("acted", [P, PACK, S], F32)
-        weighed = sb("weighed", [P, PACK, S], BF16)
-
-        def double(t, cols):
-            nc.vector.tensor_scalar(own[t][:, cols], window[t][:, cols], 2.0, None, MULT)
-
-        def activate(t, cols):
-            nc.scalar.activation(acted[:, t, cols], mixed[:, t, cols], SILU, bias=silu_bias[:], scale=0.03125)
-            nc.scalar.activation(weighed[:, t, cols], acted[:, t, cols], COPY, scale=gn_sb[:, t : t + 1])
-
-        for t in range(PACK):
-            if t > 0:
-                double(t, slice(0, S))
-            for h in range(2):
-                cols = slice(h * HALF, (h + 1) * HALF)
-                if t == 0:
-                    double(t, cols)
-                nc.vector.tensor_tensor(
-                    mixed[:, t, cols], window[t][:].indirect(nb_sb[:, 16 * h : 16 * (h + 1)]), own[t][:, cols], ADD
-                )
-                if t < PACK - 1:
-                    activate(t, cols)
-                else:
-                    for lo in range(h * HALF, (h + 1) * HALF, CHUNK):
-                        activate(t, slice(lo, lo + CHUNK))
-        w_plane = sb("w_plane", [P, N], U8, tag="own3")
+        double(0)
         nc.vector.tensor_copy(
             w_plane[:].rearrange("p (t m) -> p t m", t=PACK), w_scale_rows[:].rearrange("p (m t) -> p t m", t=PACK)
         )
+        double(1)
+        mix(0, 0)
+        mix(1, 0)
+        double(2)
+        double(3)
+        mix(2, 0)
+        mix(3, 0)
+        for t in range(PACK):
+            mix(t, 1)
 
         y_codes = sb("y_codes", [P, S], I32)
         y_scales = sb("y_scales", [P, S], U8)
         out_rows = out_0.rearrange("(p t) n -> p t n", t=PACK)
         out_words = out_1[0].rearrange("p n t -> p (n t)").bitcast(I32)
-        chunks = S // CHUNK
-        z, y, y_bf = {}, {}, {}
+        acted, z, y, y_bf = {}, {}, {}, {}
 
-        def interleave(dst, src):
-            nc.vector.tensor_copy(
-                dst.rearrange("p (c i t) -> p c t i", i=4, t=PACK), src.rearrange("p t (c i) -> p c t i", i=4)
-            )
+        def woven(tile):
+            return tile.rearrange("p (c i t) -> p c t i", i=4, t=PACK)
 
-        def weave(c):
+        def planar(tile):
+            return tile.rearrange("p t (c i) -> p c t i", i=4)
+
+        def activate(c):
+            acted[c] = sb("acted%d" % c, [P, CHUNK * PACK], F32)
+            nc.scalar.activation(woven(acted[c][:]), planar(halves[c // 2][:, :, (c % 2) * CHUNK : (c % 2 + 1) * CHUNK]), SILU, bias=silu_bias[:], scale=0.03125)
+
+        def weigh(c):
             z[c] = sb("z%d" % c, [P, CHUNK * PACK], BF16)
-            interleave(z[c][:], weighed[:, :, c * CHUNK : (c + 1) * CHUNK])
+            nc.vector.tensor_tensor(
+                z[c][:].rearrange("p (c t) -> p c t", t=PACK),
+                acted[c][:].rearrange("p (c t) -> p c t", t=PACK),
+                gn_sb[:].unsqueeze(1).to_broadcast([P, CHUNK, PACK]),
+                MULT,
+            )
 
         def second_product(c):
             z_codes = sb("z_codes%d" % c, [P, CHUNK], I32)
@@ -194,17 +200,23 @@ def tile_picked_scoremix_silu_po_kernel(
                 nc.scalar.copy(y[c][:, 2 * pair : 2 * pair + 2, :], acc[:])
             nc.sync.dma_start(out_rows[:, :, c * CHUNK : (c + 1) * CHUNK], y[c][:])
 
-        def round_result(c):
+        def round_result(c, on_scalar=False):
             y_bf[c] = sb("y_bf%d" % c, [P, CHUNK * PACK], BF16)
-            interleave(y_bf[c][:], y[c][:])
+            if on_scalar:
+                nc.scalar.copy(woven(y_bf[c][:]), planar(y[c][:]))
+            else:
+                nc.vector.tensor_copy(woven(y_bf[c][:]), planar(y[c][:]))
 
         def hand_on(c):
             cols = slice(c * CHUNK, (c + 1) * CHUNK)
             nc.vector.quantize_mx(out=y_codes[:, cols].bitcast(FP8X4), scales=y_scales[:, cols], in_=y_bf[c][:])
 
+        chunks = S // CHUNK
+        for c in range(chunks):
+            activate(c)
         for c in range(chunks + 1):
             if c < chunks:
-                weave(c)
+                weigh(c)
             if c > 0:
                 second_product(c - 1)
         for c in range(chunks + 1):

@@ -41,40 +41,40 @@ def tile_picked_scoremix_silu_po_kernel(
         def sb(name, shape, dtype, tag=None):
             return keep.tile(shape, dtype, name=name, tag=tag or name, align_bytes=64)
 
-        d_scale_table = reuse.tile([P, G], U8, name="d_scale_table", align_bytes=64, offset=4 * T)
+        d_scale_table = reuse.tile([P, G], U8, name="d_scale_table", align_bytes=64, offset=4 * T + 4 * G)
         x_scale_table = sb("x_scale_table", [P, T], U8)
-        d_table = reuse.tile([P, G], I32, name="d_table", align_bytes=64, offset=4 * T + G)
+        d_table = reuse.tile([P, G], I32, name="d_table", align_bytes=64, offset=4 * T)
         x_table = reuse.tile([P, T], I32, name="x_table", align_bytes=64, offset=0)
-        planes = sb("planes", [P, H + S], U8)
+        planes = sb("planes", [P, H + S + N], U8)
+        spread = sb("spread", [P, H + S + N], U8)
+        zero = sb("zero", [P, 1], F32)
         silu_bias = sb("silu_bias", [P, 1], F32)
 
+        nc.vector.memset(d_scale_table[:].bitcast(I32), 0)
         nc.vector.memset(x_scale_table[:].bitcast(I32), 0)
+        nc.vector.memset(zero[:], 0.0)
         nc.vector.memset(planes[:].bitcast(I32), 0)
 
-        nc.sync.dma_start(
-            d_scale_table[:].bitcast(I32), d_scales[0].bitcast(I32).unsqueeze(1).to_broadcast([16, 8, G // 4])
-        )
+        nc.scalar.dma_start(spread[:, H + S :].bitcast(I32)[0:P:8, :], w1_scales[0].bitcast(I32))
         nc.sync.dma_start(kidx_sb[:], kidx)
         nc.sync.dma_start(offs_sb[:], offs)
-        nc.sync.dma_start(nb_sb[:], nb)
         nc.sync.dma_start(d_table[:], d_words[0].rearrange("p n t -> p (n t)").bitcast(I32))
+        nc.sync.dma_start(nb_sb[:], nb)
         nc.sync.dma_start(x_table[:], x_words[0].rearrange("p n t -> p (n t)").bitcast(I32))
+        nc.scalar.dma_start(d_scale_table[:].bitcast(I32)[0:P:8, :], d_scales[0].bitcast(I32))
         nc.scalar.dma_start(x_scale_table[:].bitcast(I32)[0:P:8, :], x_scales[0].bitcast(I32))
+        nc.scalar.activation(silu_bias[:], zero[:], SILU)
 
         d_scale_picked = sb("d_scale_picked", [P, H], U8)
         x_scale_picked = sb("x_scale_picked", [P, S], U8)
-        spread = sb("spread", [P, H + S], U8)
         nc.vector.tensor_copy(d_scale_picked[:], d_scale_table[:].indirect(kidx_sb[:]))
-        zero = reuse.tile([P, 1], F32, name="zero", align_bytes=64, offset=4 * T + 2 * N)
-        nc.vector.memset(zero[:], 0.0)
-        nc.scalar.activation(silu_bias[:], zero[:], SILU)
-        w_raw = reuse.tile([P, 2 * N], U8, name="w_raw", align_bytes=64, offset=4 * T)
+        w_raw = reuse.tile([P, 2 * N], U8, name="w_raw", align_bytes=64, offset=4 * T + 4 * G)
         nc.sync.dma_start(w_raw[:].bitcast(I32), w1_words[0].bitcast(I32))
         nc.vector.tensor_copy(x_scale_picked[:], x_scale_table[:].indirect(offs_sb[:]))
         nc.vector.tensor_copy(
             spread[:, :H].rearrange("p (t m) -> p t m", t=PACK), d_scale_picked[:].rearrange("p (m t) -> p t m", t=PACK)
         )
-        nc.vector.tensor_copy(spread[:, H:].bitcast(I32), x_scale_picked[:].bitcast(I32))
+        nc.vector.tensor_copy(spread[:, H : H + S].bitcast(I32), x_scale_picked[:].bitcast(I32))
         for a in range(4):
             nc.scalar.dma_start(planes[:].bitcast(I32)[a:P:32, :], spread[:].bitcast(I32)[8 * a : P : 32, :])
 
@@ -85,14 +85,8 @@ def tile_picked_scoremix_silu_po_kernel(
             d_dealt[:].rearrange("p (t c i) -> p c t i", t=PACK, i=4),
             d_picked[:].rearrange("p (c i t) -> p c t i", t=PACK, i=4),
         )
-        gn_sb = reuse.tile([P, PACK], F32, name="gn_sb", align_bytes=64, offset=4 * T + G)
-        w_scale_rows = reuse.tile([P, N], U8, name="w_scale_rows", align_bytes=64, offset=4 * T + G + 64)
+        gn_sb = reuse.tile([P, PACK], F32, name="gn_sb", align_bytes=64, offset=4 * T)
         nc.sync.dma_start(gn_sb[:], gn.rearrange("(p t) o -> p (t o)", t=PACK))
-        for q in range(4):
-            rows = w1_scales[0].bitcast(I32)[4 * q : 4 * q + 4, :]
-            nc.sync.dma_start(
-                w_scale_rows[:].bitcast(I32)[32 * q : 32 * (q + 1), :], rows.unsqueeze(0).to_broadcast([8, 4, N // 4])
-            )
         x_picked = [
             sb("x_picked0", [P, HALF], I32, tag="x_scale_picked"),
             sb("x_picked1", [P, HALF], I32, tag="d_scale_picked"),
@@ -105,10 +99,17 @@ def tile_picked_scoremix_silu_po_kernel(
         window = [sb("window%d" % t, [P, S], F32) for t in range(PACK)]
         own = [sb("own%d" % t, [P, S], F32) for t in range(PACK)]
         banks = {}
+        for t in range(2):
+            for h in range(2):
+                banks[t, h] = psum.tile([P, HALF], F32, name="s%d%d" % (t, h), tag="bank%d" % (2 * t + h))[:]
+        whole = {}
+        for t in range(2, PACK):
+            whole[t] = psum.tile([P, S], F32, name="s%d" % t, tag="bank%d" % (2 + t))
+            for h in range(2):
+                banks[t, h] = whole[t][:, h * HALF : (h + 1) * HALF]
         for t, h in [(0, 0), (1, 0), (0, 1), (1, 1), (2, 0), (2, 1), (3, 0), (3, 1)]:
-            banks[t, h] = psum.tile([P, HALF], F32, name="s%d%d" % (t, h), tag="bank%d" % (2 * t + h))
             nc.tensor.matmul_mx(
-                out=banks[t, h][:],
+                out=banks[t, h],
                 lhsT=d_dealt[:, t * P : (t + 1) * P].bitcast(FP8X4),
                 lhsT_scale=planes[:, t * P : (t + 1) * P],
                 rhs=x_picked[h][:].bitcast(FP8X4),
@@ -116,10 +117,18 @@ def tile_picked_scoremix_silu_po_kernel(
                 start=True,
                 stop=True,
             )
-        for t, h in [(0, 0), (1, 0), (0, 1), (1, 1), (2, 0), (2, 1), (3, 0), (3, 1)]:
-            nc.scalar.copy(window[t][:, h * HALF : (h + 1) * HALF], banks[t, h][:])
-        for t in range(PACK):
-            nc.scalar.activation(own[t][:, HALF:], banks[t, 1][:], COPY, scale=2.0)
+        for t, h in [(0, 0), (1, 0), (0, 1), (1, 1)]:
+            nc.scalar.copy(window[t][:, h * HALF : (h + 1) * HALF], banks[t, h])
+
+        def double_from_bank(t, h):
+            nc.scalar.activation(own[t][:, h * HALF : (h + 1) * HALF], banks[t, h], COPY, scale=2.0)
+
+        double_from_bank(0, 1)
+        for t in range(2, PACK):
+            nc.scalar.copy(window[t][:], whole[t][:])
+            double_from_bank(t, 0)
+        for t in range(1, PACK):
+            double_from_bank(t, 1)
 
         w_dealt = reuse.tile([P, 2 * N], U8, name="w_dealt", align_bytes=64, offset=0)
         w_plane = reuse.tile([P, N], U8, name="w_plane", align_bytes=64, offset=2 * N)
@@ -142,17 +151,11 @@ def tile_picked_scoremix_silu_po_kernel(
         )
         double(0)
         nc.vector.tensor_copy(
-            w_plane[:].rearrange("p (t m) -> p t m", t=PACK), w_scale_rows[:].rearrange("p (m t) -> p t m", t=PACK)
+            w_plane[:].rearrange("p (t m) -> p t m", t=PACK), planes[:, H + S :].rearrange("p (m t) -> p t m", t=PACK)
         )
         double(1)
-        mix(0, 0)
-        mix(1, 0)
-        double(2)
-        double(3)
-        mix(2, 0)
-        mix(3, 0)
-        for t in range(PACK):
-            mix(t, 1)
+        for t, h in [(0, 0), (1, 0), (0, 1), (2, 0), (3, 0), (1, 1), (2, 1), (3, 1)]:
+            mix(t, h)
 
         y_codes = sb("y_codes", [P, S], I32)
         y_scales = sb("y_scales", [P, S], U8)
@@ -185,7 +188,7 @@ def tile_picked_scoremix_silu_po_kernel(
             nc.vector.quantize_mx(out=z_codes[:].bitcast(FP8X4), scales=z_scales[:], in_=z[c][:])
             y[c] = sb("y%d" % c, [P, PACK, CHUNK], F32)
             for pair in range(2):
-                acc = psum.tile([P, 2, CHUNK], F32, name="y%d%d" % (c, pair), tag="bank%d" % (2 * c + pair))
+                acc = psum.tile([P, 2, CHUNK], F32, name="y%d%d" % (c, pair), tag="bank%d" % ((2 * c + pair + 6) % 8))
                 for u in range(2):
                     t = 2 * pair + u
                     nc.tensor.matmul_mx(

@@ -47,29 +47,29 @@ def tile_picked_scoremix_silu_po_kernel(
         x_table = reuse.tile([P, T], I32, name="x_table", align_bytes=64, offset=0)
         planes = sb("planes", [P, H + S + N], U8)
         spread = sb("spread", [P, H + S + N], U8)
+        seed = reuse.tile([P, 32], F32, name="seed", align_bytes=64, offset=4 * T - 64)
         zero = sb("zero", [P, 1], F32)
         silu_bias = sb("silu_bias", [P, 1], F32)
 
+        nc.gpsimd.memset(x_scale_table[:].bitcast(I32), 0)
+        nc.vector.memset(seed[:], 0.0)
         nc.vector.memset(d_scale_table[:].bitcast(I32), 0)
-        nc.vector.memset(x_scale_table[:].bitcast(I32), 0)
-        nc.vector.memset(zero[:], 0.0)
+        nc.vector.tensor_reduce(zero[:], seed[:], mybir.AxisListType.X, ADD)
         nc.vector.memset(planes[:].bitcast(I32), 0)
 
         nc.scalar.dma_start(spread[:, H + S :].bitcast(I32)[0:P:8, :], w1_scales[0].bitcast(I32))
         nc.sync.dma_start(kidx_sb[:], kidx)
         nc.sync.dma_start(offs_sb[:], offs)
-        nc.sync.dma_start(d_table[:], d_words[0].rearrange("p n t -> p (n t)").bitcast(I32))
         nc.sync.dma_start(nb_sb[:], nb)
+        nc.sync.dma_start(d_scale_table[:].bitcast(I32)[0:P:8, :], d_scales[0].bitcast(I32))
+        nc.sync.dma_start(x_scale_table[:].bitcast(I32)[0:P:8, :], x_scales[0].bitcast(I32))
+        nc.sync.dma_start(d_table[:], d_words[0].rearrange("p n t -> p (n t)").bitcast(I32))
         nc.sync.dma_start(x_table[:], x_words[0].rearrange("p n t -> p (n t)").bitcast(I32))
-        nc.scalar.dma_start(d_scale_table[:].bitcast(I32)[0:P:8, :], d_scales[0].bitcast(I32))
-        nc.scalar.dma_start(x_scale_table[:].bitcast(I32)[0:P:8, :], x_scales[0].bitcast(I32))
         nc.scalar.activation(silu_bias[:], zero[:], SILU)
 
         d_scale_picked = sb("d_scale_picked", [P, H], U8)
         x_scale_picked = sb("x_scale_picked", [P, S], U8)
         nc.vector.tensor_copy(d_scale_picked[:], d_scale_table[:].indirect(kidx_sb[:]))
-        w_raw = reuse.tile([P, 2 * N], U8, name="w_raw", align_bytes=64, offset=4 * T + 4 * G)
-        nc.sync.dma_start(w_raw[:].bitcast(I32), w1_words[0].bitcast(I32))
         nc.vector.tensor_copy(x_scale_picked[:], x_scale_table[:].indirect(offs_sb[:]))
         nc.vector.tensor_copy(
             spread[:, :H].rearrange("p (t m) -> p t m", t=PACK), d_scale_picked[:].rearrange("p (m t) -> p t m", t=PACK)
@@ -77,6 +77,8 @@ def tile_picked_scoremix_silu_po_kernel(
         nc.vector.tensor_copy(spread[:, H : H + S].bitcast(I32), x_scale_picked[:].bitcast(I32))
         for a in range(4):
             nc.scalar.dma_start(planes[:].bitcast(I32)[a:P:32, :], spread[:].bitcast(I32)[8 * a : P : 32, :])
+        w_raw = sb("w_raw", [P, 2 * N], U8, tag="x_scale_picked")
+        nc.sync.dma_start(w_raw[:].bitcast(I32), w1_words[0].bitcast(I32))
 
         d_picked = sb("d_picked", [P, H], I32, tag="x_scale_table")
         d_dealt = sb("d_dealt", [P, H], I32)
@@ -88,7 +90,7 @@ def tile_picked_scoremix_silu_po_kernel(
         gn_sb = reuse.tile([P, PACK], F32, name="gn_sb", align_bytes=64, offset=4 * T)
         nc.sync.dma_start(gn_sb[:], gn.rearrange("(p t) o -> p (t o)", t=PACK))
         x_picked = [
-            sb("x_picked0", [P, HALF], I32, tag="x_scale_picked"),
+            sb("x_picked0", [P, HALF], I32),
             sb("x_picked1", [P, HALF], I32, tag="d_scale_picked"),
         ]
         for h in range(2):

@@ -51,9 +51,9 @@ def tile_picked_scoremix_silu_po_kernel(
         zero = sb("zero", [P, 1], F32)
         silu_bias = sb("silu_bias", [P, 1], F32)
 
-        nc.gpsimd.memset(x_scale_table[:].bitcast(I32), 0)
-        nc.vector.memset(seed[:], 0.0)
         nc.vector.memset(d_scale_table[:].bitcast(I32), 0)
+        nc.vector.memset(seed[:], 0.0)
+        nc.vector.memset(x_scale_table[:].bitcast(I32), 0)
         nc.vector.tensor_reduce(zero[:], seed[:], mybir.AxisListType.X, ADD)
         nc.vector.memset(planes[:].bitcast(I32), 0)
 

@@ -47,17 +47,18 @@ def tile_picked_scoremix_silu_po_kernel(
         x_table = reuse.tile([P, T], I32, name="x_table", align_bytes=64, offset=0)
         planes = sb("planes", [P, H + S + N], U8)
         spread = sb("spread", [P, H + S + N], U8)
+        w_scale_raw = sb("w_scale_raw", [P, N], U8)
         seed = reuse.tile([P, 32], F32, name="seed", align_bytes=64, offset=4 * T - 64)
         zero = sb("zero", [P, 1], F32)
         silu_bias = sb("silu_bias", [P, 1], F32)
 
+        nc.vector.memset(w_scale_raw[:].bitcast(I32), 0)
         nc.vector.memset(d_scale_table[:].bitcast(I32), 0)
         nc.vector.memset(seed[:], 0.0)
         nc.vector.memset(x_scale_table[:].bitcast(I32), 0)
         nc.vector.tensor_reduce(zero[:], seed[:], mybir.AxisListType.X, ADD)
-        nc.vector.memset(planes[:].bitcast(I32), 0)
 
-        nc.scalar.dma_start(spread[:, H + S :].bitcast(I32)[0:P:8, :], w1_scales[0].bitcast(I32))
+        nc.scalar.dma_start(w_scale_raw[:].bitcast(I32)[0:P:8, :], w1_scales[0].bitcast(I32))
         nc.sync.dma_start(kidx_sb[:], kidx)
         nc.sync.dma_start(offs_sb[:], offs)
         nc.sync.dma_start(nb_sb[:], nb)
@@ -67,6 +68,9 @@ def tile_picked_scoremix_silu_po_kernel(
         nc.sync.dma_start(x_table[:], x_words[0].rearrange("p n t -> p (n t)").bitcast(I32))
         nc.scalar.activation(silu_bias[:], zero[:], SILU)
 
+        nc.vector.tensor_copy(
+            spread[:, H + S :].rearrange("p (t m) -> p t m", t=PACK), w_scale_raw[:].rearrange("p (m t) -> p t m", t=PACK)
+        )
         d_scale_picked = sb("d_scale_picked", [P, H], U8)
         x_scale_picked = sb("x_scale_picked", [P, S], U8)
         nc.vector.tensor_copy(d_scale_picked[:], d_scale_table[:].indirect(kidx_sb[:]))
@@ -82,11 +86,16 @@ def tile_picked_scoremix_silu_po_kernel(
 
         d_picked = sb("d_picked", [P, H], I32, tag="x_scale_table")
         d_dealt = sb("d_dealt", [P, H], I32)
-        nc.vector.tensor_copy(d_picked[:].bitcast(U32), d_table[:].bitcast(U32).indirect(kidx_sb[:]))
-        nc.vector.tensor_copy(
-            d_dealt[:].rearrange("p (t c i) -> p c t i", t=PACK, i=4),
-            d_picked[:].rearrange("p (c i t) -> p c t i", t=PACK, i=4),
-        )
+        for h in range(2):
+            nc.vector.tensor_copy(
+                d_picked[:, h * HALF : (h + 1) * HALF].bitcast(U32),
+                d_table[:].bitcast(U32).indirect(kidx_sb[:, h * 16 : (h + 1) * 16]),
+            )
+        for h in range(2):
+            nc.vector.tensor_copy(
+                d_dealt[:].rearrange("p (t c i) -> p c t i", t=PACK, i=4)[:, h * 16 : (h + 1) * 16],
+                d_picked[:].rearrange("p (c i t) -> p c t i", t=PACK, i=4)[:, h * 16 : (h + 1) * 16],
+            )
         gn_sb = reuse.tile([P, PACK], F32, name="gn_sb", align_bytes=64, offset=4 * T)
         nc.sync.dma_start(gn_sb[:], gn.rearrange("(p t) o -> p (t o)", t=PACK))
         x_picked = [
@@ -99,7 +108,7 @@ def tile_picked_scoremix_silu_po_kernel(
             )
 
         window = [sb("window%d" % t, [P, S], F32) for t in range(PACK)]
-        own = [sb("own%d" % t, [P, S], F32) for t in range(PACK)]
+        own = {}
         banks = {}
         for t in range(2):
             for h in range(2):
@@ -123,27 +132,28 @@ def tile_picked_scoremix_silu_po_kernel(
             nc.scalar.copy(window[t][:, h * HALF : (h + 1) * HALF], banks[t, h])
 
         def double_from_bank(t, h):
-            nc.scalar.activation(own[t][:, h * HALF : (h + 1) * HALF], banks[t, h], COPY, scale=2.0)
+            own[t, h] = sb("own%d%d" % (t, h), [P, HALF], F32, tag="own30" if t == 3 else None)
+            nc.scalar.activation(own[t, h][:], banks[t, h], COPY, scale=2.0)
 
         double_from_bank(0, 1)
         for t in range(2, PACK):
             nc.scalar.copy(window[t][:], whole[t][:])
             double_from_bank(t, 0)
-        for t in range(1, PACK):
+        for t in range(1, PACK - 1):
             double_from_bank(t, 1)
 
         w_dealt = reuse.tile([P, 2 * N], U8, name="w_dealt", align_bytes=64, offset=0)
-        w_plane = reuse.tile([P, N], U8, name="w_plane", align_bytes=64, offset=2 * N)
         halves = [sb("mixed%d" % h, [P, PACK, HALF], F32) for h in range(2)]
 
         def double(t):
-            nc.vector.tensor_scalar(own[t][:, :HALF], window[t][:, :HALF], 2.0, None, MULT)
+            own[t, 0] = sb("own%d0" % t, [P, HALF], F32)
+            nc.vector.tensor_scalar(own[t, 0][:], window[t][:, :HALF], 2.0, None, MULT)
 
         def mix(t, h):
             nc.vector.tensor_tensor(
                 halves[h][:, t, :],
                 window[t][:].indirect(nb_sb[:, 16 * h : 16 * (h + 1)]),
-                own[t][:, h * HALF : (h + 1) * HALF],
+                own[t, h][:],
                 ADD,
             )
 
@@ -152,14 +162,10 @@ def tile_picked_scoremix_silu_po_kernel(
             w_raw[:].rearrange("p (m t b) -> p t m b", t=PACK, b=2),
         )
         double(0)
-        nc.vector.tensor_copy(
-            w_plane[:].rearrange("p (t m) -> p t m", t=PACK), planes[:, H + S :].rearrange("p (m t) -> p t m", t=PACK)
-        )
         double(1)
-        for t, h in [(0, 0), (1, 0), (0, 1), (2, 0), (3, 0), (1, 1), (2, 1), (3, 1)]:
+        for t, h in [(0, 0), (1, 0), (0, 1), (2, 0), (3, 0), (1, 1), (2, 1)]:
             mix(t, h)
 
-        y_codes = sb("y_codes", [P, S], I32)
         y_scales = sb("y_scales", [P, S], U8)
         out_rows = out_0.rearrange("(p t) n -> p t n", t=PACK)
         out_words = out_1[0].rearrange("p n t -> p (n t)").bitcast(I32)
@@ -171,16 +177,36 @@ def tile_picked_scoremix_silu_po_kernel(
         def planar(tile):
             return tile.rearrange("p t (c i) -> p c t i", i=4)
 
+        warm = psum.tile([P, S], F32, name="warm", tag="bank5")
+
+        def warm_up(codes, scales):
+            nc.tensor.matmul_mx(
+                out=warm[:],
+                lhsT=codes.bitcast(FP8X4),
+                lhsT_scale=scales,
+                rhs=d_dealt[:].bitcast(FP8X4),
+                rhs_scale=planes[:, :H],
+                start=True,
+                stop=True,
+            )
+
         def activate(c):
-            acted[c] = sb("acted%d" % c, [P, CHUNK * PACK], F32)
-            nc.scalar.activation(woven(acted[c][:]), planar(halves[c // 2][:, :, (c % 2) * CHUNK : (c % 2 + 1) * CHUNK]), SILU, bias=silu_bias[:], scale=0.03125)
+            acted[c] = sb("acted%d" % c, [P, PACK, CHUNK], F32)
+            nc.scalar.activation(acted[c][:], halves[c // 2][:, :, (c % 2) * CHUNK : (c % 2 + 1) * CHUNK], SILU, bias=silu_bias[:], scale=0.03125)
+
+        def activate_second_half():
+            late = sb("acted_late", [P, PACK, HALF], F32)
+            for t in range(PACK):
+                nc.scalar.activation(late[:, t, :], halves[1][:, t, :], SILU, bias=silu_bias[:], scale=0.03125)
+            for c in range(2, 4):
+                acted[c] = late[:, :, (c % 2) * CHUNK : (c % 2 + 1) * CHUNK]
 
         def weigh(c):
-            z[c] = sb("z%d" % c, [P, CHUNK * PACK], BF16)
+            z[c] = sb("z%d" % c, [P, CHUNK * PACK], BF16, tag="z1" if c == 3 else None)
             nc.vector.tensor_tensor(
-                z[c][:].rearrange("p (c t) -> p c t", t=PACK),
-                acted[c][:].rearrange("p (c t) -> p c t", t=PACK),
-                gn_sb[:].unsqueeze(1).to_broadcast([P, CHUNK, PACK]),
+                woven(z[c][:]),
+                planar(acted[c][:]),
+                gn_sb[:].unsqueeze(1).unsqueeze(3).to_broadcast([P, CHUNK // 4, PACK, 4]),
                 MULT,
             )
 
@@ -196,17 +222,19 @@ def tile_picked_scoremix_silu_po_kernel(
                     nc.tensor.matmul_mx(
                         out=acc[:, u, :],
                         lhsT=w_dealt[:, 2 * t * P : 2 * (t + 1) * P].bitcast(FP4X4),
-                        lhsT_scale=w_plane[:, t * P : (t + 1) * P],
+                        lhsT_scale=planes[:, H + S + t * P : H + S + (t + 1) * P],
                         rhs=z_codes[:].bitcast(FP8X4),
                         rhs_scale=z_scales[:],
                         start=True,
                         stop=True,
                     )
                 nc.scalar.copy(y[c][:, 2 * pair : 2 * pair + 2, :], acc[:])
+            if c == 0:
+                warm_up(z_codes[:], z_scales[:])
             nc.sync.dma_start(out_rows[:, :, c * CHUNK : (c + 1) * CHUNK], y[c][:])
 
         def round_result(c, on_scalar=False):
-            y_bf[c] = sb("y_bf%d" % c, [P, CHUNK * PACK], BF16)
+            y_bf[c] = sb("y_bf%d" % c, [P, CHUNK * PACK], BF16, tag="z2" if c == 0 else "acted_late" if c == 1 else None)
             if on_scalar:
                 nc.scalar.copy(woven(y_bf[c][:]), planar(y[c][:]))
             else:
@@ -217,18 +245,28 @@ def tile_picked_scoremix_silu_po_kernel(
             nc.vector.quantize_mx(out=y_codes[:, cols].bitcast(FP8X4), scales=y_scales[:, cols], in_=y_bf[c][:])
 
         chunks = S // CHUNK
-        for c in range(chunks):
-            activate(c)
-        for c in range(chunks + 1):
-            if c < chunks:
-                weigh(c)
-            if c > 0:
-                second_product(c - 1)
-        for c in range(chunks + 1):
-            if c < chunks:
-                round_result(c)
-            if c > 0:
+        activate(0)
+        double_from_bank(3, 1)
+        warm_up(d_dealt[:, :P], planes[:, :P])
+        weigh(0)
+        mix(3, 1)
+        activate(1)
+        activate_second_half()
+        second_product(0)
+        weigh(1)
+        weigh(2)
+        second_product(1)
+        second_product(2)
+        weigh(3)
+        round_result(0)
+        second_product(3)
+        y_codes = sb("y_codes", [P, S], I32)
+        hand_on(0)
+        for c in range(1, chunks):
+            round_result(c)
+            if c > 1:
                 hand_on(c - 1)
+        hand_on(chunks - 1)
         nc.sync.dma_start(out_words[:, : S - CHUNK], y_codes[:, : S - CHUNK])
         nc.sync.dma_start(out_words[:, S - CHUNK :], y_codes[:, S - CHUNK :])
         for q in range(4):

@@ -46,7 +46,6 @@ def tile_picked_scoremix_silu_po_kernel(
         d_table = reuse.tile([P, G], I32, name="d_table", align_bytes=64, offset=4 * T)
         x_table = reuse.tile([P, T], I32, name="x_table", align_bytes=64, offset=0)
         planes = sb("planes", [P, H + S + N], U8)
-        spread = sb("spread", [P, H + S + N], U8)
         w_scale_raw = sb("w_scale_raw", [P, N], U8)
         seed = reuse.tile([P, 32], F32, name="seed", align_bytes=64, offset=4 * T - 64)
         zero = sb("zero", [P, 1], F32)
@@ -69,18 +68,18 @@ def tile_picked_scoremix_silu_po_kernel(
         nc.scalar.activation(silu_bias[:], zero[:], SILU)
 
         nc.vector.tensor_copy(
-            spread[:, H + S :].rearrange("p (t m) -> p t m", t=PACK), w_scale_raw[:].rearrange("p (m t) -> p t m", t=PACK)
+            planes[:, H + S :].rearrange("p (t m) -> p t m", t=PACK), w_scale_raw[:].rearrange("p (m t) -> p t m", t=PACK)
         )
         d_scale_picked = sb("d_scale_picked", [P, H], U8)
         x_scale_picked = sb("x_scale_picked", [P, S], U8)
         nc.vector.tensor_copy(d_scale_picked[:], d_scale_table[:].indirect(kidx_sb[:]))
         nc.vector.tensor_copy(x_scale_picked[:], x_scale_table[:].indirect(offs_sb[:]))
         nc.vector.tensor_copy(
-            spread[:, :H].rearrange("p (t m) -> p t m", t=PACK), d_scale_picked[:].rearrange("p (m t) -> p t m", t=PACK)
+            planes[:, :H].rearrange("p (t m) -> p t m", t=PACK), d_scale_picked[:].rearrange("p (m t) -> p t m", t=PACK)
         )
-        nc.vector.tensor_copy(spread[:, H : H + S].bitcast(I32), x_scale_picked[:].bitcast(I32))
-        for a in range(4):
-            nc.scalar.dma_start(planes[:].bitcast(I32)[a:P:32, :], spread[:].bitcast(I32)[8 * a : P : 32, :])
+        nc.vector.tensor_copy(planes[:, H : H + S].bitcast(I32), x_scale_picked[:].bitcast(I32))
+        for a in range(1, 4):
+            nc.scalar.dma_start(planes[:].bitcast(I32)[a:P:32, :], planes[:].bitcast(I32)[8 * a : P : 32, :])
         w_raw = sb("w_raw", [P, 2 * N], U8, tag="x_scale_picked")
         nc.sync.dma_start(w_raw[:].bitcast(I32), w1_words[0].bitcast(I32))
 
@@ -142,7 +141,7 @@ def tile_picked_scoremix_silu_po_kernel(
         for t in range(1, PACK - 1):
             double_from_bank(t, 1)
 
-        w_dealt = reuse.tile([P, 2 * N], U8, name="w_dealt", align_bytes=64, offset=0)
+        w_dealt = sb("w_dealt", [P, 2 * N], U8)
         halves = [sb("mixed%d" % h, [P, PACK, HALF], F32) for h in range(2)]
 
         def double(t):
@@ -177,27 +176,15 @@ def tile_picked_scoremix_silu_po_kernel(
         def planar(tile):
             return tile.rearrange("p t (c i) -> p c t i", i=4)
 
-        warm = psum.tile([P, S], F32, name="warm", tag="bank5")
-
-        def warm_up(codes, scales):
-            nc.tensor.matmul_mx(
-                out=warm[:],
-                lhsT=codes.bitcast(FP8X4),
-                lhsT_scale=scales,
-                rhs=d_dealt[:].bitcast(FP8X4),
-                rhs_scale=planes[:, :H],
-                start=True,
-                stop=True,
-            )
-
         def activate(c):
             acted[c] = sb("acted%d" % c, [P, PACK, CHUNK], F32)
             nc.scalar.activation(acted[c][:], halves[c // 2][:, :, (c % 2) * CHUNK : (c % 2 + 1) * CHUNK], SILU, bias=silu_bias[:], scale=0.03125)
 
         def activate_second_half():
             late = sb("acted_late", [P, PACK, HALF], F32)
-            for t in range(PACK):
-                nc.scalar.activation(late[:, t, :], halves[1][:, t, :], SILU, bias=silu_bias[:], scale=0.03125)
+            pieces = [(t, 0, HALF) for t in range(PACK - 1)] + [(PACK - 1, 0, CHUNK), (PACK - 1, CHUNK, HALF)]
+            for t, lo, hi in pieces:
+                nc.scalar.activation(late[:, t, lo:hi], halves[1][:, t, lo:hi], SILU, bias=silu_bias[:], scale=0.03125)
             for c in range(2, 4):
                 acted[c] = late[:, :, (c % 2) * CHUNK : (c % 2 + 1) * CHUNK]
 
@@ -229,8 +216,6 @@ def tile_picked_scoremix_silu_po_kernel(
                         stop=True,
                     )
                 nc.scalar.copy(y[c][:, 2 * pair : 2 * pair + 2, :], acc[:])
-            if c == 0:
-                warm_up(z_codes[:], z_scales[:])
             nc.sync.dma_start(out_rows[:, :, c * CHUNK : (c + 1) * CHUNK], y[c][:])
 
         def round_result(c, on_scalar=False):
@@ -247,7 +232,6 @@ def tile_picked_scoremix_silu_po_kernel(
         chunks = S // CHUNK
         activate(0)
         double_from_bank(3, 1)
-        warm_up(d_dealt[:, :P], planes[:, :P])
         weigh(0)
         mix(3, 1)
         activate(1)
@@ -261,11 +245,9 @@ def tile_picked_scoremix_silu_po_kernel(
         round_result(0)
         second_product(3)
         y_codes = sb("y_codes", [P, S], I32)
-        hand_on(0)
         for c in range(1, chunks):
             round_result(c)
-            if c > 1:
-                hand_on(c - 1)
+            hand_on(c - 1)
         hand_on(chunks - 1)
         nc.sync.dma_start(out_words[:, : S - CHUNK], y_codes[:, : S - CHUNK])
         nc.sync.dma_start(out_words[:, S - CHUNK :], y_codes[:, S - CHUNK :])

@@ -20,8 +20,18 @@ SILU = mybir.ActivationFunctionType.Silu
 
 P = 128
 PACK = 4
+GROUP = 16
+BLOCK_ROWS = 8
+QUADRANT = 32
+RUN = 4
 HALF = S // 2
+HALF_LIST = HALF // GROUP
 CHUNK = 128
+CHUNKS = S // CHUNK
+BANKS = 8
+EARLY = 2
+LAST_TILE = PACK - 1
+SILU_SCALE = 0.0625 * 0.5
 
 
 def tile_picked_scoremix_silu_po_kernel(
@@ -31,23 +41,35 @@ def tile_picked_scoremix_silu_po_kernel(
     with ExitStack() as ctx:
         lists = ctx.enter_context(tc.tile_pool(name="lists", bufs=1))
         keep = ctx.enter_context(tc.tile_pool(name="keep", bufs=1))
-        reuse = ctx.enter_context(tc.tile_pool(name="reuse", bufs=1))
+        placed = ctx.enter_context(tc.tile_pool(name="placed", bufs=1))
         psum = ctx.enter_context(tc.psum_pool(name="psum", bufs=1))
 
-        kidx_sb = lists.tile([P, H // 16], U16, name="kidx_sb")
-        offs_sb = lists.tile([P, S // 16], U16, name="offs_sb")
-        nb_sb = lists.tile([P, S // 16], U16, name="nb_sb")
+        kidx_sb = lists.tile([P, H // GROUP], U16, name="kidx_sb")
+        offs_sb = lists.tile([P, S // GROUP], U16, name="offs_sb")
+        nb_sb = lists.tile([P, S // GROUP], U16, name="nb_sb")
 
-        def sb(name, shape, dtype, tag=None):
-            return keep.tile(shape, dtype, name=name, tag=tag or name, align_bytes=64)
+        def sb(name, shape, dtype, slot_of=None):
+            return keep.tile(shape, dtype, name=name, tag=slot_of or name, align_bytes=64)
 
-        d_scale_table = reuse.tile([P, G], U8, name="d_scale_table", align_bytes=64, offset=4 * T + 4 * G)
+        def place(name, shape, dtype, offset):
+            return placed.tile(shape, dtype, name=name, align_bytes=64, offset=offset)
+
+        def list_half(entries, h):
+            return entries[:, h * HALF_LIST : (h + 1) * HALF_LIST]
+
+        def deal_bytes(dealt, plain):
+            nc.vector.tensor_copy(
+                dealt.rearrange("p (t m) -> p t m", t=PACK), plain.rearrange("p (m t) -> p t m", t=PACK)
+            )
+
+        d_offset = 4 * T
+        d_scale_table = place("d_scale_table", [P, G], U8, d_offset + 4 * G)
         x_scale_table = sb("x_scale_table", [P, T], U8)
-        d_table = reuse.tile([P, G], I32, name="d_table", align_bytes=64, offset=4 * T)
-        x_table = reuse.tile([P, T], I32, name="x_table", align_bytes=64, offset=0)
+        d_table = place("d_table", [P, G], I32, d_offset)
+        x_table = place("x_table", [P, T], I32, 0)
         planes = sb("planes", [P, H + S + N], U8)
         w_scale_raw = sb("w_scale_raw", [P, N], U8)
-        seed = reuse.tile([P, 32], F32, name="seed", align_bytes=64, offset=4 * T - 64)
+        seed = place("seed", [P, 32], F32, d_offset - 64)
         zero = sb("zero", [P, 1], F32)
         silu_bias = sb("silu_bias", [P, 1], F32)
 
@@ -57,200 +79,210 @@ def tile_picked_scoremix_silu_po_kernel(
         nc.vector.memset(x_scale_table[:].bitcast(I32), 0)
         nc.vector.tensor_reduce(zero[:], seed[:], mybir.AxisListType.X, ADD)
 
-        nc.scalar.dma_start(w_scale_raw[:].bitcast(I32)[0:P:8, :], w1_scales[0].bitcast(I32))
+        nc.scalar.dma_start(w_scale_raw[:].bitcast(I32)[0:P:BLOCK_ROWS, :], w1_scales[0].bitcast(I32))
         nc.sync.dma_start(kidx_sb[:], kidx)
         nc.sync.dma_start(offs_sb[:], offs)
         nc.sync.dma_start(nb_sb[:], nb)
-        nc.sync.dma_start(d_scale_table[:].bitcast(I32)[0:P:8, :], d_scales[0].bitcast(I32))
-        nc.sync.dma_start(x_scale_table[:].bitcast(I32)[0:P:8, :], x_scales[0].bitcast(I32))
+        nc.sync.dma_start(d_scale_table[:].bitcast(I32)[0:P:BLOCK_ROWS, :], d_scales[0].bitcast(I32))
+        nc.sync.dma_start(x_scale_table[:].bitcast(I32)[0:P:BLOCK_ROWS, :], x_scales[0].bitcast(I32))
         nc.sync.dma_start(d_table[:], d_words[0].rearrange("p n t -> p (n t)").bitcast(I32))
         nc.sync.dma_start(x_table[:], x_words[0].rearrange("p n t -> p (n t)").bitcast(I32))
         nc.scalar.activation(silu_bias[:], zero[:], SILU)
 
-        nc.vector.tensor_copy(
-            planes[:, H + S :].rearrange("p (t m) -> p t m", t=PACK), w_scale_raw[:].rearrange("p (m t) -> p t m", t=PACK)
-        )
+        d_plane, x_plane, w_plane = planes[:, :H], planes[:, H : H + S], planes[:, H + S :]
+        deal_bytes(w_plane, w_scale_raw[:])
         d_scale_picked = sb("d_scale_picked", [P, H], U8)
         x_scale_picked = sb("x_scale_picked", [P, S], U8)
         nc.vector.tensor_copy(d_scale_picked[:], d_scale_table[:].indirect(kidx_sb[:]))
         nc.vector.tensor_copy(x_scale_picked[:], x_scale_table[:].indirect(offs_sb[:]))
-        nc.vector.tensor_copy(
-            planes[:, :H].rearrange("p (t m) -> p t m", t=PACK), d_scale_picked[:].rearrange("p (m t) -> p t m", t=PACK)
-        )
-        nc.vector.tensor_copy(planes[:, H : H + S].bitcast(I32), x_scale_picked[:].bitcast(I32))
-        for a in range(1, 4):
-            nc.scalar.dma_start(planes[:].bitcast(I32)[a:P:32, :], planes[:].bitcast(I32)[8 * a : P : 32, :])
-        w_raw = sb("w_raw", [P, 2 * N], U8, tag="x_scale_picked")
+        deal_bytes(d_plane, d_scale_picked[:])
+        nc.vector.tensor_copy(x_plane.bitcast(I32), x_scale_picked[:].bitcast(I32))
+        for a in range(1, QUADRANT // BLOCK_ROWS):
+            nc.scalar.dma_start(
+                planes[:].bitcast(I32)[a:P:QUADRANT, :], planes[:].bitcast(I32)[BLOCK_ROWS * a : P : QUADRANT, :]
+            )
+        w_raw = sb("w_raw", [P, 2 * N], U8, slot_of="x_scale_picked")
         nc.sync.dma_start(w_raw[:].bitcast(I32), w1_words[0].bitcast(I32))
 
-        d_picked = sb("d_picked", [P, H], I32, tag="x_scale_table")
+        d_picked = sb("d_picked", [P, H], I32, slot_of="x_scale_table")
         d_dealt = sb("d_dealt", [P, H], I32)
         for h in range(2):
             nc.vector.tensor_copy(
                 d_picked[:, h * HALF : (h + 1) * HALF].bitcast(U32),
-                d_table[:].bitcast(U32).indirect(kidx_sb[:, h * 16 : (h + 1) * 16]),
+                d_table[:].bitcast(U32).indirect(list_half(kidx_sb, h)),
             )
+        runs = HALF // (PACK * RUN)
         for h in range(2):
             nc.vector.tensor_copy(
-                d_dealt[:].rearrange("p (t c i) -> p c t i", t=PACK, i=4)[:, h * 16 : (h + 1) * 16],
-                d_picked[:].rearrange("p (c i t) -> p c t i", t=PACK, i=4)[:, h * 16 : (h + 1) * 16],
+                d_dealt[:].rearrange("p (t c i) -> p c t i", t=PACK, i=RUN)[:, h * runs : (h + 1) * runs],
+                d_picked[:].rearrange("p (c i t) -> p c t i", t=PACK, i=RUN)[:, h * runs : (h + 1) * runs],
             )
-        gn_sb = reuse.tile([P, PACK], F32, name="gn_sb", align_bytes=64, offset=4 * T)
+        gn_sb = place("gn_sb", [P, PACK], F32, d_offset)
         nc.sync.dma_start(gn_sb[:], gn.rearrange("(p t) o -> p (t o)", t=PACK))
         x_picked = [
             sb("x_picked0", [P, HALF], I32),
-            sb("x_picked1", [P, HALF], I32, tag="d_scale_picked"),
+            sb("x_picked1", [P, HALF], I32, slot_of="d_scale_picked"),
         ]
         for h in range(2):
             nc.vector.tensor_copy(
-                x_picked[h][:].bitcast(U32), x_table[:].bitcast(U32).indirect(offs_sb[:, h * 16 : (h + 1) * 16])
+                x_picked[h][:].bitcast(U32), x_table[:].bitcast(U32).indirect(list_half(offs_sb, h))
             )
 
         window = [sb("window%d" % t, [P, S], F32) for t in range(PACK)]
-        own = {}
-        banks = {}
-        for t in range(2):
+        scores = {}
+        for t in range(EARLY):
             for h in range(2):
-                banks[t, h] = psum.tile([P, HALF], F32, name="s%d%d" % (t, h), tag="bank%d" % (2 * t + h))[:]
+                scores[t, h] = psum.tile([P, HALF], F32, name="s%d%d" % (t, h), tag="bank%d" % (2 * t + h))[:]
         whole = {}
-        for t in range(2, PACK):
-            whole[t] = psum.tile([P, S], F32, name="s%d" % t, tag="bank%d" % (2 + t))
+        for t in range(EARLY, PACK):
+            whole[t] = psum.tile([P, S], F32, name="s%d" % t, tag="bank%d" % (EARLY + t))
             for h in range(2):
-                banks[t, h] = whole[t][:, h * HALF : (h + 1) * HALF]
-        for t, h in [(0, 0), (1, 0), (0, 1), (1, 1), (2, 0), (2, 1), (3, 0), (3, 1)]:
+                scores[t, h] = whole[t][:, h * HALF : (h + 1) * HALF]
+        early_passes = [(t, h) for h in range(2) for t in range(EARLY)]
+        late_passes = [(t, h) for t in range(EARLY, PACK) for h in range(2)]
+        for t, h in early_passes + late_passes:
             nc.tensor.matmul_mx(
-                out=banks[t, h],
+                out=scores[t, h],
                 lhsT=d_dealt[:, t * P : (t + 1) * P].bitcast(FP8X4),
-                lhsT_scale=planes[:, t * P : (t + 1) * P],
+                lhsT_scale=d_plane[:, t * P : (t + 1) * P],
                 rhs=x_picked[h][:].bitcast(FP8X4),
-                rhs_scale=planes[:, H + h * HALF : H + (h + 1) * HALF],
+                rhs_scale=x_plane[:, h * HALF : (h + 1) * HALF],
                 start=True,
                 stop=True,
             )
-        for t, h in [(0, 0), (1, 0), (0, 1), (1, 1)]:
-            nc.scalar.copy(window[t][:, h * HALF : (h + 1) * HALF], banks[t, h])
+        for t, h in early_passes:
+            nc.scalar.copy(window[t][:, h * HALF : (h + 1) * HALF], scores[t, h])
 
-        def double_from_bank(t, h):
-            own[t, h] = sb("own%d%d" % (t, h), [P, HALF], F32, tag="own30" if t == 3 else None)
-            nc.scalar.activation(own[t, h][:], banks[t, h], COPY, scale=2.0)
+        doubled = {}
 
-        double_from_bank(0, 1)
-        for t in range(2, PACK):
+        def double_on_scalar(t, h, slot_of=None):
+            doubled[t, h] = sb("doubled%d%d" % (t, h), [P, HALF], F32, slot_of)
+            nc.scalar.activation(doubled[t, h][:], scores[t, h], COPY, scale=2.0)
+
+        def double_on_vector(t):
+            doubled[t, 0] = sb("doubled%d0" % t, [P, HALF], F32)
+            nc.vector.tensor_scalar(doubled[t, 0][:], window[t][:, :HALF], 2.0, None, MULT)
+
+        double_on_scalar(0, 1)
+        for t in range(EARLY, PACK):
             nc.scalar.copy(window[t][:], whole[t][:])
-            double_from_bank(t, 0)
-        for t in range(1, PACK - 1):
-            double_from_bank(t, 1)
+            double_on_scalar(t, 0)
+        for t in range(1, LAST_TILE):
+            double_on_scalar(t, 1)
 
         w_dealt = sb("w_dealt", [P, 2 * N], U8)
-        halves = [sb("mixed%d" % h, [P, PACK, HALF], F32) for h in range(2)]
-
-        def double(t):
-            own[t, 0] = sb("own%d0" % t, [P, HALF], F32)
-            nc.vector.tensor_scalar(own[t, 0][:], window[t][:, :HALF], 2.0, None, MULT)
+        mixed = [sb("mixed%d" % h, [P, PACK, HALF], F32) for h in range(2)]
 
         def mix(t, h):
-            nc.vector.tensor_tensor(
-                halves[h][:, t, :],
-                window[t][:].indirect(nb_sb[:, 16 * h : 16 * (h + 1)]),
-                own[t, h][:],
-                ADD,
-            )
+            nc.vector.tensor_tensor(mixed[h][:, t, :], window[t][:].indirect(list_half(nb_sb, h)), doubled[t, h][:], ADD)
 
         nc.vector.tensor_copy(
-            w_dealt[:].rearrange("p (t m b) -> p t m b", t=PACK, b=2),
-            w_raw[:].rearrange("p (m t b) -> p t m b", t=PACK, b=2),
+            w_dealt[:].bitcast(U16).rearrange("p (t m) -> p t m", t=PACK),
+            w_raw[:].bitcast(U16).rearrange("p (m t) -> p t m", t=PACK),
         )
-        double(0)
-        double(1)
-        for t, h in [(0, 0), (1, 0), (0, 1), (2, 0), (3, 0), (1, 1), (2, 1)]:
-            mix(t, h)
+        for t in range(EARLY):
+            double_on_vector(t)
+        for t in range(EARLY):
+            mix(t, 0)
+        mix(0, 1)
+        for t in range(EARLY, PACK):
+            mix(t, 0)
+        for t in range(1, LAST_TILE):
+            mix(t, 1)
 
         y_scales = sb("y_scales", [P, S], U8)
         out_rows = out_0.rearrange("(p t) n -> p t n", t=PACK)
         out_words = out_1[0].rearrange("p n t -> p (n t)").bitcast(I32)
         acted, z, y, y_bf = {}, {}, {}, {}
 
-        def woven(tile):
-            return tile.rearrange("p (c i t) -> p c t i", i=4, t=PACK)
+        def woven(ap):
+            return ap.rearrange("p (c i t) -> p c t i", i=RUN, t=PACK)
 
-        def planar(tile):
-            return tile.rearrange("p t (c i) -> p c t i", i=4)
+        def planar(ap):
+            return ap.rearrange("p t (c i) -> p c t i", i=RUN)
 
-        def activate(c):
-            acted[c] = sb("acted%d" % c, [P, PACK, CHUNK], F32)
-            nc.scalar.activation(acted[c][:], halves[c // 2][:, :, (c % 2) * CHUNK : (c % 2 + 1) * CHUNK], SILU, bias=silu_bias[:], scale=0.03125)
+        def silu(out, in_):
+            nc.scalar.activation(out, in_, SILU, bias=silu_bias[:], scale=SILU_SCALE)
+
+        def activate_chunk(c):
+            acted[c] = sb("acted%d" % c, [P, PACK, CHUNK], F32)[:]
+            silu(acted[c], mixed[0][:, :, c * CHUNK : (c + 1) * CHUNK])
 
         def activate_second_half():
             late = sb("acted_late", [P, PACK, HALF], F32)
-            pieces = [(t, 0, HALF) for t in range(PACK - 1)] + [(PACK - 1, 0, CHUNK), (PACK - 1, CHUNK, HALF)]
-            for t, lo, hi in pieces:
-                nc.scalar.activation(late[:, t, lo:hi], halves[1][:, t, lo:hi], SILU, bias=silu_bias[:], scale=0.03125)
-            for c in range(2, 4):
-                acted[c] = late[:, :, (c % 2) * CHUNK : (c % 2 + 1) * CHUNK]
+            for t in range(LAST_TILE):
+                silu(late[:, t, :], mixed[1][:, t, :])
+            for u in range(2):
+                cols = slice(u * CHUNK, (u + 1) * CHUNK)
+                silu(late[:, LAST_TILE, cols], mixed[1][:, LAST_TILE, cols])
+                acted[2 + u] = late[:, :, cols]
 
-        def weigh(c):
-            z[c] = sb("z%d" % c, [P, CHUNK * PACK], BF16, tag="z1" if c == 3 else None)
-            nc.vector.tensor_tensor(
-                woven(z[c][:]),
-                planar(acted[c][:]),
-                gn_sb[:].unsqueeze(1).unsqueeze(3).to_broadcast([P, CHUNK // 4, PACK, 4]),
-                MULT,
-            )
+        def weigh(c, slot_of=None):
+            z[c] = sb("z%d" % c, [P, CHUNK * PACK], BF16, slot_of)
+            weights = gn_sb[:].unsqueeze(1).unsqueeze(3).to_broadcast([P, CHUNK // RUN, PACK, RUN])
+            nc.vector.tensor_tensor(woven(z[c][:]), planar(acted[c]), weights, MULT)
 
-        def second_product(c):
+        def second_product(c, store_by_bank=False):
+            cols = slice(c * CHUNK, (c + 1) * CHUNK)
             z_codes = sb("z_codes%d" % c, [P, CHUNK], I32)
             z_scales = sb("z_scales%d" % c, [P, CHUNK], U8)
             nc.vector.quantize_mx(out=z_codes[:].bitcast(FP8X4), scales=z_scales[:], in_=z[c][:])
             y[c] = sb("y%d" % c, [P, PACK, CHUNK], F32)
             for pair in range(2):
-                acc = psum.tile([P, 2, CHUNK], F32, name="y%d%d" % (c, pair), tag="bank%d" % ((2 * c + pair + 6) % 8))
+                tiles = slice(2 * pair, 2 * pair + 2)
+                bank = (EARLY + PACK + 2 * c + pair) % BANKS
+                acc = psum.tile([P, 2, CHUNK], F32, name="y%d%d" % (c, pair), tag="bank%d" % bank)
                 for u in range(2):
                     t = 2 * pair + u
                     nc.tensor.matmul_mx(
                         out=acc[:, u, :],
                         lhsT=w_dealt[:, 2 * t * P : 2 * (t + 1) * P].bitcast(FP4X4),
-                        lhsT_scale=planes[:, H + S + t * P : H + S + (t + 1) * P],
+                        lhsT_scale=w_plane[:, t * P : (t + 1) * P],
                         rhs=z_codes[:].bitcast(FP8X4),
                         rhs_scale=z_scales[:],
                         start=True,
                         stop=True,
                     )
-                nc.scalar.copy(y[c][:, 2 * pair : 2 * pair + 2, :], acc[:])
-            nc.sync.dma_start(out_rows[:, :, c * CHUNK : (c + 1) * CHUNK], y[c][:])
+                nc.scalar.copy(y[c][:, tiles, :], acc[:])
+                if store_by_bank:
+                    nc.sync.dma_start(out_rows[:, tiles, cols], y[c][:, tiles, :])
+            if not store_by_bank:
+                nc.sync.dma_start(out_rows[:, :, cols], y[c][:])
 
-        def round_result(c, on_scalar=False):
-            y_bf[c] = sb("y_bf%d" % c, [P, CHUNK * PACK], BF16, tag="z2" if c == 0 else "acted_late" if c == 1 else None)
-            if on_scalar:
-                nc.scalar.copy(woven(y_bf[c][:]), planar(y[c][:]))
-            else:
-                nc.vector.tensor_copy(woven(y_bf[c][:]), planar(y[c][:]))
+        def round_result(c, slot_of=None):
+            y_bf[c] = sb("y_bf%d" % c, [P, CHUNK * PACK], BF16, slot_of)
+            nc.vector.tensor_copy(woven(y_bf[c][:]), planar(y[c][:]))
 
-        def hand_on(c):
+        def quantise_result(c):
             cols = slice(c * CHUNK, (c + 1) * CHUNK)
             nc.vector.quantize_mx(out=y_codes[:, cols].bitcast(FP8X4), scales=y_scales[:, cols], in_=y_bf[c][:])
 
-        chunks = S // CHUNK
-        activate(0)
-        double_from_bank(3, 1)
+        activate_chunk(0)
+        double_on_scalar(LAST_TILE, 1, slot_of="doubled%d0" % LAST_TILE)
         weigh(0)
-        mix(3, 1)
-        activate(1)
+        mix(LAST_TILE, 1)
+        activate_chunk(1)
         activate_second_half()
         second_product(0)
         weigh(1)
         weigh(2)
-        second_product(1)
+        second_product(1, store_by_bank=True)
         second_product(2)
-        weigh(3)
-        round_result(0)
+        weigh(3, slot_of="z1")
+        round_result(0, slot_of="z2")
         second_product(3)
         y_codes = sb("y_codes", [P, S], I32)
-        for c in range(1, chunks):
+        round_result(1, slot_of="acted_late")
+        quantise_result(0)
+        for c in range(2, CHUNKS):
             round_result(c)
-            hand_on(c - 1)
-        hand_on(chunks - 1)
+            quantise_result(c - 1)
+        quantise_result(CHUNKS - 1)
+
         nc.sync.dma_start(out_words[:, : S - CHUNK], y_codes[:, : S - CHUNK])
         nc.sync.dma_start(out_words[:, S - CHUNK :], y_codes[:, S - CHUNK :])
-        for q in range(4):
+        for q in range(P // QUADRANT):
             queue = nc.sync if q % 2 == 0 else nc.scalar
-            queue.dma_start(out_2[0].bitcast(I32)[4 * q : 4 * q + 4, :], y_scales[:].bitcast(I32)[32 * q : 32 * q + 4, :])
+            queue.dma_start(
+                out_2[0].bitcast(I32)[4 * q : 4 * q + 4, :], y_scales[:].bitcast(I32)[QUADRANT * q : QUADRANT * q + 4, :]
+            )

@@ -153,42 +153,44 @@ def tile_picked_scoremix_silu_po_kernel(
         for t, h in early_passes:
             nc.scalar.copy(window[t][:, h * HALF : (h + 1) * HALF], scores[t, h])
 
-        doubled = {}
-
-        def double_on_scalar(t, h, slot_of=None):
-            doubled[t, h] = sb("doubled%d%d" % (t, h), [P, HALF], F32, slot_of)
-            nc.scalar.activation(doubled[t, h][:], scores[t, h], COPY, scale=2.0)
-
-        def double_on_vector(t):
-            doubled[t, 0] = sb("doubled%d0" % t, [P, HALF], F32)
-            nc.vector.tensor_scalar(doubled[t, 0][:], window[t][:, :HALF], 2.0, None, MULT)
-
-        double_on_scalar(0, 1)
         for t in range(EARLY, PACK):
             nc.scalar.copy(window[t][:], whole[t][:])
-            double_on_scalar(t, 0)
-        for t in range(1, LAST_TILE):
-            double_on_scalar(t, 1)
 
+        doubled = {}
+        fetched = {}
         w_dealt = sb("w_dealt", [P, 2 * N], U8)
         mixed = [sb("mixed%d" % h, [P, PACK, HALF], F32) for h in range(2)]
 
+        def double(t, halves):
+            both = sb("doubled%d" % t, [P, halves * HALF], F32)
+            nc.vector.tensor_scalar(both[:], window[t][:, : halves * HALF], 2.0, None, MULT)
+            for h in range(halves):
+                doubled[t, h] = both[:, h * HALF : (h + 1) * HALF]
+
         def mix(t, h):
-            nc.vector.tensor_tensor(mixed[h][:, t, :], window[t][:].indirect(list_half(nb_sb, h)), doubled[t, h][:], ADD)
+            nc.vector.tensor_tensor(mixed[h][:, t, :], window[t][:].indirect(list_half(nb_sb, h)), doubled[t, h], ADD)
+
+        def fetch(t):
+            fetched[t] = sb("fetched%d" % t, [P, HALF], F32)
+            nc.scalar.activation(fetched[t][:], window[t][:].indirect(list_half(nb_sb, 1)), COPY)
+
+        def add_fetched(t):
+            nc.vector.scalar_tensor_tensor(mixed[1][:, t, :], window[t][:, HALF:], 2.0, fetched[t][:], MULT, ADD)
 
         nc.vector.tensor_copy(
             w_dealt[:].bitcast(U16).rearrange("p (t m) -> p t m", t=PACK),
             w_raw[:].bitcast(U16).rearrange("p (m t) -> p t m", t=PACK),
         )
         for t in range(EARLY):
-            double_on_vector(t)
+            double(t, 1)
         for t in range(EARLY):
             mix(t, 0)
-        mix(0, 1)
+        double(2, 1)
+        double(LAST_TILE, 2)
         for t in range(EARLY, PACK):
             mix(t, 0)
-        for t in range(1, LAST_TILE):
-            mix(t, 1)
+        for t in range(LAST_TILE):
+            fetch(t)
 
         y_scales = sb("y_scales", [P, S], U8)
         out_rows = out_0.rearrange("(p t) n -> p t n", t=PACK)
@@ -258,10 +260,11 @@ def tile_picked_scoremix_silu_po_kernel(
             nc.vector.quantize_mx(out=y_codes[:, cols].bitcast(FP8X4), scales=y_scales[:, cols], in_=y_bf[c][:])
 
         activate_chunk(0)
-        double_on_scalar(LAST_TILE, 1, slot_of="doubled%d0" % LAST_TILE)
+        activate_chunk(1)
+        for t in range(LAST_TILE):
+            add_fetched(t)
         weigh(0)
         mix(LAST_TILE, 1)
-        activate_chunk(1)
         activate_second_half()
         second_product(0)
         weigh(1)

@@ -29,8 +29,8 @@ HALF_LIST = HALF // GROUP
 CHUNK = 128
 CHUNKS = S // CHUNK
 BANKS = 8
-EARLY = 2
-LAST_TILE = PACK - 1
+OWN = (0, 1)
+FETCHED = (2, 3)
 SILU_SCALE = 0.0625 * 0.5
 
 
@@ -42,6 +42,7 @@ def tile_picked_scoremix_silu_po_kernel(
         lists = ctx.enter_context(tc.tile_pool(name="lists", bufs=1))
         keep = ctx.enter_context(tc.tile_pool(name="keep", bufs=1))
         placed = ctx.enter_context(tc.tile_pool(name="placed", bufs=1))
+        held = ctx.enter_context(tc.tile_pool(name="held", bufs=1))
         psum = ctx.enter_context(tc.psum_pool(name="psum", bufs=1))
 
         kidx_sb = lists.tile([P, H // GROUP], U16, name="kidx_sb")
@@ -129,20 +130,11 @@ def tile_picked_scoremix_silu_po_kernel(
             )
 
         window = [sb("window%d" % t, [P, S], F32) for t in range(PACK)]
-        scores = {}
-        for t in range(EARLY):
-            for h in range(2):
-                scores[t, h] = psum.tile([P, HALF], F32, name="s%d%d" % (t, h), tag="bank%d" % (2 * t + h))[:]
-        whole = {}
-        for t in range(EARLY, PACK):
-            whole[t] = psum.tile([P, S], F32, name="s%d" % t, tag="bank%d" % (EARLY + t))
-            for h in range(2):
-                scores[t, h] = whole[t][:, h * HALF : (h + 1) * HALF]
-        early_passes = [(t, h) for h in range(2) for t in range(EARLY)]
-        late_passes = [(t, h) for t in range(EARLY, PACK) for h in range(2)]
-        for t, h in early_passes + late_passes:
+        passes = [(t, h) for h in range(2) for t in OWN] + [(t, h) for t in FETCHED for h in range(2)]
+        for n, (t, h) in enumerate(passes):
+            scores = psum.tile([P, HALF], F32, name="s%d%d" % (t, h), tag="bank%d" % n)
             nc.tensor.matmul_mx(
-                out=scores[t, h],
+                out=scores[:],
                 lhsT=d_dealt[:, t * P : (t + 1) * P].bitcast(FP8X4),
                 lhsT_scale=d_plane[:, t * P : (t + 1) * P],
                 rhs=x_picked[h][:].bitcast(FP8X4),
@@ -150,52 +142,48 @@ def tile_picked_scoremix_silu_po_kernel(
                 start=True,
                 stop=True,
             )
-        for t, h in early_passes:
-            nc.scalar.copy(window[t][:, h * HALF : (h + 1) * HALF], scores[t, h])
+            nc.scalar.copy(window[t][:, h * HALF : (h + 1) * HALF], scores[:])
 
-        for t in range(EARLY, PACK):
-            nc.scalar.copy(window[t][:], whole[t][:])
-
-        doubled = {}
-        fetched = {}
         w_dealt = sb("w_dealt", [P, 2 * N], U8)
-        mixed = [sb("mixed%d" % h, [P, PACK, HALF], F32) for h in range(2)]
-
-        def double(t, halves):
-            both = sb("doubled%d" % t, [P, halves * HALF], F32)
-            nc.vector.tensor_scalar(both[:], window[t][:, : halves * HALF], 2.0, None, MULT)
-            for h in range(halves):
-                doubled[t, h] = both[:, h * HALF : (h + 1) * HALF]
-
-        def mix(t, h):
-            nc.vector.tensor_tensor(mixed[h][:, t, :], window[t][:].indirect(list_half(nb_sb, h)), doubled[t, h], ADD)
-
-        def fetch(t):
-            fetched[t] = sb("fetched%d" % t, [P, HALF], F32)
-            nc.scalar.activation(fetched[t][:], window[t][:].indirect(list_half(nb_sb, 1)), COPY)
-
-        def add_fetched(t):
-            nc.vector.scalar_tensor_tensor(mixed[1][:, t, :], window[t][:, HALF:], 2.0, fetched[t][:], MULT, ADD)
-
         nc.vector.tensor_copy(
             w_dealt[:].bitcast(U16).rearrange("p (t m) -> p t m", t=PACK),
             w_raw[:].bitcast(U16).rearrange("p (m t) -> p t m", t=PACK),
         )
-        for t in range(EARLY):
-            double(t, 1)
-        for t in range(EARLY):
-            mix(t, 0)
-        double(2, 1)
-        double(LAST_TILE, 2)
-        for t in range(EARLY, PACK):
-            mix(t, 0)
-        for t in range(LAST_TILE):
-            fetch(t)
+
+        def hold(name, shape, dtype, offset):
+            return held.tile(shape, dtype, name=name, align_bytes=64, offset=offset)
+
+        act_bytes = 4 * PACK * CHUNK
+        fetched = {
+            (2, 0): hold("fetched20", [P, HALF], F32, 2 * act_bytes - 128),
+            (3, 0): sb("fetched30", [P, HALF], F32),
+            (2, 1): sb("fetched21", [P, HALF], F32),
+        }
+        doubled = {(t, h): sb("doubled%d%d" % (t, h), [P, HALF], F32) for t in OWN for h in range(2)}
+        mixed_first = sb("mixed_first", [P, PACK, HALF], F32)
+        mixed = {(t, 0): mixed_first[:, t, :] for t in range(PACK)}
+        mixed[0, 1] = sb("mixed01", [P, HALF], F32)[:]
+        mixed_late = sb("mixed_late", [P, 2, HALF], F32)
+        mixed[2, 1], mixed[3, 1] = mixed_late[:, 0, :], mixed_late[:, 1, :]
+
+        def double(t, h):
+            nc.vector.tensor_scalar(doubled[t, h][:], window[t][:, h * HALF : (h + 1) * HALF], 2.0, None, MULT)
+
+        def mix(t, h):
+            nc.vector.tensor_tensor(mixed[t, h], window[t][:].indirect(list_half(nb_sb, h)), doubled[t, h][:], ADD)
+
+        def fetch(t, h):
+            nc.scalar.activation(fetched[t, h][:], window[t][:].indirect(list_half(nb_sb, h)), COPY)
+
+        def add_fetched(t, h):
+            own = window[t][:, h * HALF : (h + 1) * HALF]
+            nc.vector.scalar_tensor_tensor(mixed[t, h], own, 2.0, fetched[t, h][:], MULT, ADD)
 
         y_scales = sb("y_scales", [P, S], U8)
+        y_codes = sb("y_codes", [P, S], I32)
         out_rows = out_0.rearrange("(p t) n -> p t n", t=PACK)
         out_words = out_1[0].rearrange("p n t -> p (n t)").bitcast(I32)
-        acted, z, y, y_bf = {}, {}, {}, {}
+        acted, z, y, y_bf, acc = {}, {}, {}, {}, {}
 
         def woven(ap):
             return ap.rearrange("p (c i t) -> p c t i", i=RUN, t=PACK)
@@ -206,38 +194,26 @@ def tile_picked_scoremix_silu_po_kernel(
         def silu(out, in_):
             nc.scalar.activation(out, in_, SILU, bias=silu_bias[:], scale=SILU_SCALE)
 
-        def activate_chunk(c):
-            acted[c] = sb("acted%d" % c, [P, PACK, CHUNK], F32)[:]
-            silu(acted[c], mixed[0][:, :, c * CHUNK : (c + 1) * CHUNK])
-
-        def activate_second_half():
-            late = sb("acted_late", [P, PACK, HALF], F32)
-            for t in range(LAST_TILE):
-                silu(late[:, t, :], mixed[1][:, t, :])
-            for u in range(2):
-                cols = slice(u * CHUNK, (u + 1) * CHUNK)
-                silu(late[:, LAST_TILE, cols], mixed[1][:, LAST_TILE, cols])
-                acted[2 + u] = late[:, :, cols]
-
         def weigh(c, slot_of=None):
             z[c] = sb("z%d" % c, [P, CHUNK * PACK], BF16, slot_of)
             weights = gn_sb[:].unsqueeze(1).unsqueeze(3).to_broadcast([P, CHUNK // RUN, PACK, RUN])
-            nc.vector.tensor_tensor(woven(z[c][:]), planar(acted[c]), weights, MULT)
+            nc.vector.tensor_tensor(woven(z[c][:]), planar(acted[c][:]), weights, MULT)
 
-        def second_product(c, store_by_bank=False):
-            cols = slice(c * CHUNK, (c + 1) * CHUNK)
+        free_banks = list(range(BANKS)) * 2
+
+        def second_product(c, banks):
             z_codes = sb("z_codes%d" % c, [P, CHUNK], I32)
             z_scales = sb("z_scales%d" % c, [P, CHUNK], U8)
             nc.vector.quantize_mx(out=z_codes[:].bitcast(FP8X4), scales=z_scales[:], in_=z[c][:])
-            y[c] = sb("y%d" % c, [P, PACK, CHUNK], F32)
-            for pair in range(2):
-                tiles = slice(2 * pair, 2 * pair + 2)
-                bank = (EARLY + PACK + 2 * c + pair) % BANKS
-                acc = psum.tile([P, 2, CHUNK], F32, name="y%d%d" % (c, pair), tag="bank%d" % bank)
-                for u in range(2):
-                    t = 2 * pair + u
+            share = PACK // banks
+            acc[c] = []
+            for b in range(banks):
+                bank = psum.tile([P, share, CHUNK], F32, name="y%d%d" % (c, b), tag="bank%d" % free_banks.pop(0))
+                acc[c].append(bank)
+                for u in range(share):
+                    t = share * b + u
                     nc.tensor.matmul_mx(
-                        out=acc[:, u, :],
+                        out=bank[:, u, :],
                         lhsT=w_dealt[:, 2 * t * P : 2 * (t + 1) * P].bitcast(FP4X4),
                         lhsT_scale=w_plane[:, t * P : (t + 1) * P],
                         rhs=z_codes[:].bitcast(FP8X4),
@@ -245,11 +221,13 @@ def tile_picked_scoremix_silu_po_kernel(
                         start=True,
                         stop=True,
                     )
-                nc.scalar.copy(y[c][:, tiles, :], acc[:])
-                if store_by_bank:
-                    nc.sync.dma_start(out_rows[:, tiles, cols], y[c][:, tiles, :])
-            if not store_by_bank:
-                nc.sync.dma_start(out_rows[:, :, cols], y[c][:])
+
+        def empty(c):
+            y[c] = sb("y%d" % c, [P, PACK, CHUNK], F32)
+            share = PACK // len(acc[c])
+            for b, bank in enumerate(acc[c]):
+                nc.scalar.copy(y[c][:, share * b : share * (b + 1), :], bank[:])
+            nc.sync.dma_start(out_rows[:, :, c * CHUNK : (c + 1) * CHUNK], y[c][:])
 
         def round_result(c, slot_of=None):
             y_bf[c] = sb("y_bf%d" % c, [P, CHUNK * PACK], BF16, slot_of)
@@ -259,31 +237,56 @@ def tile_picked_scoremix_silu_po_kernel(
             cols = slice(c * CHUNK, (c + 1) * CHUNK)
             nc.vector.quantize_mx(out=y_codes[:, cols].bitcast(FP8X4), scales=y_scales[:, cols], in_=y_bf[c][:])
 
-        activate_chunk(0)
-        activate_chunk(1)
-        for t in range(LAST_TILE):
-            add_fetched(t)
+        double(0, 0)
+        double(1, 0)
+        double(0, 1)
+        mix(0, 0)
+        double(1, 1)
+        mix(1, 0)
+        mix(0, 1)
+        fetch(2, 0)
+        fetch(3, 0)
+        add_fetched(2, 0)
+        add_fetched(3, 0)
+        mixed[1, 1] = hold("mixed11", [P, HALF], F32, 2 * act_bytes)[:]
+        mix(1, 1)
+        fetch(2, 1)
+        add_fetched(2, 1)
+        acted[0] = hold("acted0", [P, PACK, CHUNK], F32, act_bytes - 64)
+        silu(acted[0][:, :2, :], mixed_first[:, :2, :CHUNK])
+        silu(acted[0][:, 2:, :], mixed_first[:, 2:, :CHUNK])
+        fetched[3, 1] = sb("fetched31", [P, HALF], F32, "fetched30")
+        fetch(3, 1)
         weigh(0)
-        mix(LAST_TILE, 1)
-        activate_second_half()
-        second_product(0)
+        add_fetched(3, 1)
+        second_product(0, 1)
+        acted[1] = sb("acted1", [P, PACK, CHUNK], F32)
+        silu(acted[1][:], mixed_first[:, :, CHUNK:])
         weigh(1)
+        for u in range(2):
+            cols = slice(u * CHUNK, (u + 1) * CHUNK)
+            acted[2 + u] = hold("acted%d" % (2 + u), [P, PACK, CHUNK], F32, u * act_bytes)
+            for t in OWN:
+                silu(acted[2 + u][:, t, :], mixed[t, 1][:, cols])
+            silu(acted[2 + u][:, 2:, :], mixed_late[:, :, cols])
         weigh(2)
-        second_product(1, store_by_bank=True)
-        second_product(2)
-        weigh(3, slot_of="z1")
-        round_result(0, slot_of="z2")
-        second_product(3)
-        y_codes = sb("y_codes", [P, S], I32)
-        round_result(1, slot_of="acted_late")
+        second_product(1, 2)
+        weigh(3)
+        second_product(2, 2)
+        second_product(3, 4)
+        for c in range(CHUNKS):
+            empty(c)
+        round_result(0)
         quantise_result(0)
-        for c in range(2, CHUNKS):
-            round_result(c)
-            quantise_result(c - 1)
-        quantise_result(CHUNKS - 1)
+        round_result(1)
+        round_result(2)
+        quantise_result(1)
+        round_result(3)
+        quantise_result(2)
+        quantise_result(3)
 
-        nc.sync.dma_start(out_words[:, : S - CHUNK], y_codes[:, : S - CHUNK])
-        nc.sync.dma_start(out_words[:, S - CHUNK :], y_codes[:, S - CHUNK :])
+        for first, last in ((0, HALF), (HALF, S)):
+            nc.sync.dma_start(out_words[:, first:last], y_codes[:, first:last])
         for q in range(P // QUADRANT):
             queue = nc.sync if q % 2 == 0 else nc.scalar
             queue.dma_start(

@@ -194,10 +194,11 @@ def tile_picked_scoremix_silu_po_kernel(
         def silu(out, in_):
             nc.scalar.activation(out, in_, SILU, bias=silu_bias[:], scale=SILU_SCALE)
 
-        def weigh(c, slot_of=None):
-            z[c] = sb("z%d" % c, [P, CHUNK * PACK], BF16, slot_of)
-            weights = gn_sb[:].unsqueeze(1).unsqueeze(3).to_broadcast([P, CHUNK // RUN, PACK, RUN])
-            nc.vector.tensor_tensor(woven(z[c][:]), planar(acted[c][:]), weights, MULT)
+        def weigh(c, first=0, last=CHUNK // RUN):
+            if first == 0:
+                z[c] = sb("z%d" % c, [P, CHUNK * PACK], BF16)
+            weights = gn_sb[:].unsqueeze(1).unsqueeze(3).to_broadcast([P, last - first, PACK, RUN])
+            nc.vector.tensor_tensor(woven(z[c][:])[:, first:last], planar(acted[c][:])[:, first:last], weights, MULT)
 
         free_banks = list(range(BANKS)) * 2
 
@@ -269,21 +270,19 @@ def tile_picked_scoremix_silu_po_kernel(
             for t in OWN:
                 silu(acted[2 + u][:, t, :], mixed[t, 1][:, cols])
             silu(acted[2 + u][:, 2:, :], mixed_late[:, :, cols])
-        weigh(2)
-        second_product(1, 2)
-        weigh(3)
-        second_product(2, 2)
-        second_product(3, 4)
-        for c in range(CHUNKS):
-            empty(c)
+        middle = CHUNK // RUN // 2
+        for c in (2, 3):
+            weigh(c, last=middle)
+            second_product(c - 1, 2)
+            weigh(c, first=middle)
+        empty(0)
         round_result(0)
+        second_product(3, 2)
         quantise_result(0)
-        round_result(1)
-        round_result(2)
-        quantise_result(1)
-        round_result(3)
-        quantise_result(2)
-        quantise_result(3)
+        for c in range(1, CHUNKS):
+            empty(c)
+            round_result(c)
+            quantise_result(c)
 
         for first, last in ((0, HALF), (HALF, S)):
             nc.sync.dma_start(out_words[:, first:last], y_codes[:, first:last])

@@ -58,8 +58,8 @@ def tile_picked_scoremix_silu_po_kernel(
         def list_half(entries, h):
             return entries[:, h * HALF_LIST : (h + 1) * HALF_LIST]
 
-        def deal_bytes(dealt, plain):
-            nc.vector.tensor_copy(
+        def deal_bytes(engine, dealt, plain):
+            engine.tensor_copy(
                 dealt.rearrange("p (t m) -> p t m", t=PACK), plain.rearrange("p (m t) -> p t m", t=PACK)
             )
 
@@ -74,7 +74,7 @@ def tile_picked_scoremix_silu_po_kernel(
         zero = sb("zero", [P, 1], F32)
         silu_bias = sb("silu_bias", [P, 1], F32)
 
-        nc.vector.memset(w_scale_raw[:].bitcast(I32), 0)
+        nc.gpsimd.memset(w_scale_raw[:].bitcast(I32), 0)
         nc.vector.memset(d_scale_table[:].bitcast(I32), 0)
         nc.vector.memset(seed[:], 0.0)
         nc.vector.memset(x_scale_table[:].bitcast(I32), 0)
@@ -91,12 +91,12 @@ def tile_picked_scoremix_silu_po_kernel(
         nc.scalar.activation(silu_bias[:], zero[:], SILU)
 
         d_plane, x_plane, w_plane = planes[:, :H], planes[:, H : H + S], planes[:, H + S :]
-        deal_bytes(w_plane, w_scale_raw[:])
+        deal_bytes(nc.gpsimd, w_plane, w_scale_raw[:])
         d_scale_picked = sb("d_scale_picked", [P, H], U8)
         x_scale_picked = sb("x_scale_picked", [P, S], U8)
         nc.vector.tensor_copy(d_scale_picked[:], d_scale_table[:].indirect(kidx_sb[:]))
         nc.vector.tensor_copy(x_scale_picked[:], x_scale_table[:].indirect(offs_sb[:]))
-        deal_bytes(d_plane, d_scale_picked[:])
+        deal_bytes(nc.vector, d_plane, d_scale_picked[:])
         nc.vector.tensor_copy(x_plane.bitcast(I32), x_scale_picked[:].bitcast(I32))
         for a in range(1, QUADRANT // BLOCK_ROWS):
             nc.scalar.dma_start(

@@ -106,17 +106,18 @@ def tile_picked_scoremix_silu_po_kernel(
         nc.sync.dma_start(w_raw[:].bitcast(I32), w1_words[0].bitcast(I32))
 
         d_picked = sb("d_picked", [P, H], I32, slot_of="x_scale_table")
-        d_dealt = sb("d_dealt", [P, H], I32)
+        d_dealt = [sb("d_dealt_own", [P, 2, P], I32), place("d_dealt_fetched", [P, 2, P], I32, 0)]
         for h in range(2):
             nc.vector.tensor_copy(
                 d_picked[:, h * HALF : (h + 1) * HALF].bitcast(U32),
                 d_table[:].bitcast(U32).indirect(list_half(kidx_sb, h)),
             )
         runs = HALF // (PACK * RUN)
+        d_plain = d_picked[:].rearrange("p (c i t) -> p c t i", t=PACK, i=RUN)
         for h in range(2):
             nc.vector.tensor_copy(
-                d_dealt[:].rearrange("p (t c i) -> p c t i", t=PACK, i=RUN)[:, h * runs : (h + 1) * runs],
-                d_picked[:].rearrange("p (c i t) -> p c t i", t=PACK, i=RUN)[:, h * runs : (h + 1) * runs],
+                d_dealt[0][:].rearrange("p t (c i) -> p c t i", i=RUN)[:, h * runs : (h + 1) * runs],
+                d_plain[:, h * runs : (h + 1) * runs, :2],
             )
         gn_sb = place("gn_sb", [P, PACK], F32, d_offset)
         nc.sync.dma_start(gn_sb[:], gn.rearrange("(p t) o -> p (t o)", t=PACK))
@@ -129,13 +130,15 @@ def tile_picked_scoremix_silu_po_kernel(
                 x_picked[h][:].bitcast(U32), x_table[:].bitcast(U32).indirect(list_half(offs_sb, h))
             )
 
+        nc.vector.tensor_copy(d_dealt[1][:].rearrange("p t (c i) -> p c t i", i=RUN), d_plain[:, :, 2:])
+
         window = [sb("window%d" % t, [P, S], F32) for t in range(PACK)]
         passes = [(t, h) for h in range(2) for t in OWN] + [(t, h) for t in FETCHED for h in range(2)]
         for n, (t, h) in enumerate(passes):
             scores = psum.tile([P, HALF], F32, name="s%d%d" % (t, h), tag="bank%d" % n)
             nc.tensor.matmul_mx(
                 out=scores[:],
-                lhsT=d_dealt[:, t * P : (t + 1) * P].bitcast(FP8X4),
+                lhsT=d_dealt[t // 2][:, t % 2, :].bitcast(FP8X4),
                 lhsT_scale=d_plane[:, t * P : (t + 1) * P],
                 rhs=x_picked[h][:].bitcast(FP8X4),
                 rhs_scale=x_plane[:, h * HALF : (h + 1) * HALF],
@@ -277,12 +280,12 @@ def tile_picked_scoremix_silu_po_kernel(
             weigh(c, first=middle)
         empty(0)
         round_result(0)
-        second_product(3, 2)
-        quantise_result(0)
+        second_product(3, PACK)
         for c in range(1, CHUNKS):
             empty(c)
-            round_result(c)
-            quantise_result(c)
+            round_result(c, slot_of="z_codes3" if c == 2 else None)
+            quantise_result(c - 1)
+        quantise_result(CHUNKS - 1)
 
         for first, last in ((0, HALF), (HALF, S)):
             nc.sync.dma_start(out_words[:, first:last], y_codes[:, first:last])

@@ -58,8 +58,8 @@ def tile_picked_scoremix_silu_po_kernel(
         def list_half(entries, h):
             return entries[:, h * HALF_LIST : (h + 1) * HALF_LIST]
 
-        def deal_bytes(engine, dealt, plain):
-            engine.tensor_copy(
+        def deal_bytes(dealt, plain):
+            nc.vector.tensor_copy(
                 dealt.rearrange("p (t m) -> p t m", t=PACK), plain.rearrange("p (m t) -> p t m", t=PACK)
             )
 
@@ -74,16 +74,16 @@ def tile_picked_scoremix_silu_po_kernel(
         zero = sb("zero", [P, 1], F32)
         silu_bias = sb("silu_bias", [P, 1], F32)
 
-        nc.gpsimd.memset(w_scale_raw[:].bitcast(I32), 0)
+        nc.vector.memset(w_scale_raw[:].bitcast(I32), 0)
         nc.vector.memset(d_scale_table[:].bitcast(I32), 0)
         nc.vector.memset(seed[:], 0.0)
         nc.vector.memset(x_scale_table[:].bitcast(I32), 0)
         nc.vector.tensor_reduce(zero[:], seed[:], mybir.AxisListType.X, ADD)
 
-        nc.scalar.dma_start(w_scale_raw[:].bitcast(I32)[0:P:BLOCK_ROWS, :], w1_scales[0].bitcast(I32))
         nc.sync.dma_start(kidx_sb[:], kidx)
         nc.sync.dma_start(offs_sb[:], offs)
         nc.sync.dma_start(nb_sb[:], nb)
+        nc.sync.dma_start(w_scale_raw[:].bitcast(I32)[0:P:BLOCK_ROWS, :], w1_scales[0].bitcast(I32))
         nc.sync.dma_start(d_scale_table[:].bitcast(I32)[0:P:BLOCK_ROWS, :], d_scales[0].bitcast(I32))
         nc.sync.dma_start(x_scale_table[:].bitcast(I32)[0:P:BLOCK_ROWS, :], x_scales[0].bitcast(I32))
         nc.sync.dma_start(d_table[:], d_words[0].rearrange("p n t -> p (n t)").bitcast(I32))
@@ -91,12 +91,12 @@ def tile_picked_scoremix_silu_po_kernel(
         nc.scalar.activation(silu_bias[:], zero[:], SILU)
 
         d_plane, x_plane, w_plane = planes[:, :H], planes[:, H : H + S], planes[:, H + S :]
-        deal_bytes(nc.gpsimd, w_plane, w_scale_raw[:])
+        deal_bytes(w_plane, w_scale_raw[:])
         d_scale_picked = sb("d_scale_picked", [P, H], U8)
         x_scale_picked = sb("x_scale_picked", [P, S], U8)
         nc.vector.tensor_copy(d_scale_picked[:], d_scale_table[:].indirect(kidx_sb[:]))
         nc.vector.tensor_copy(x_scale_picked[:], x_scale_table[:].indirect(offs_sb[:]))
-        deal_bytes(nc.vector, d_plane, d_scale_picked[:])
+        deal_bytes(d_plane, d_scale_picked[:])
         nc.vector.tensor_copy(x_plane.bitcast(I32), x_scale_picked[:].bitcast(I32))
         for a in range(1, QUADRANT // BLOCK_ROWS):
             nc.scalar.dma_start(

@@ -24,6 +24,7 @@ GROUP = 16
 BLOCK_ROWS = 8
 QUADRANT = 32
 RUN = 4
+WALK = 2
 HALF = S // 2
 HALF_LIST = HALF // GROUP
 CHUNK = 128
@@ -80,10 +81,10 @@ def tile_picked_scoremix_silu_po_kernel(
         nc.vector.memset(x_scale_table[:].bitcast(I32), 0)
         nc.vector.tensor_reduce(zero[:], seed[:], mybir.AxisListType.X, ADD)
 
+        nc.scalar.dma_start(w_scale_raw[:].bitcast(I32)[0:P:BLOCK_ROWS, :], w1_scales[0].bitcast(I32))
         nc.sync.dma_start(kidx_sb[:], kidx)
         nc.sync.dma_start(offs_sb[:], offs)
         nc.sync.dma_start(nb_sb[:], nb)
-        nc.sync.dma_start(w_scale_raw[:].bitcast(I32)[0:P:BLOCK_ROWS, :], w1_scales[0].bitcast(I32))
         nc.sync.dma_start(d_scale_table[:].bitcast(I32)[0:P:BLOCK_ROWS, :], d_scales[0].bitcast(I32))
         nc.sync.dma_start(x_scale_table[:].bitcast(I32)[0:P:BLOCK_ROWS, :], x_scales[0].bitcast(I32))
         nc.sync.dma_start(d_table[:], d_words[0].rearrange("p n t -> p (n t)").bitcast(I32))
@@ -189,18 +190,18 @@ def tile_picked_scoremix_silu_po_kernel(
         acted, z, y, y_bf, acc = {}, {}, {}, {}, {}
 
         def woven(ap):
-            return ap.rearrange("p (c i t) -> p c t i", i=RUN, t=PACK)
+            return ap.rearrange("p (c i t) -> p c t i", i=WALK, t=PACK)
 
         def planar(ap):
-            return ap.rearrange("p t (c i) -> p c t i", i=RUN)
+            return ap.rearrange("p t (c i) -> p c t i", i=WALK)
 
         def silu(out, in_):
             nc.scalar.activation(out, in_, SILU, bias=silu_bias[:], scale=SILU_SCALE)
 
-        def weigh(c, first=0, last=CHUNK // RUN):
+        def weigh(c, first=0, last=CHUNK // WALK):
             if first == 0:
                 z[c] = sb("z%d" % c, [P, CHUNK * PACK], BF16)
-            weights = gn_sb[:].unsqueeze(1).unsqueeze(3).to_broadcast([P, last - first, PACK, RUN])
+            weights = gn_sb[:].unsqueeze(1).unsqueeze(3).to_broadcast([P, last - first, PACK, WALK])
             nc.vector.tensor_tensor(woven(z[c][:])[:, first:last], planar(acted[c][:])[:, first:last], weights, MULT)
 
         free_banks = list(range(BANKS)) * 2
@@ -273,7 +274,7 @@ def tile_picked_scoremix_silu_po_kernel(
             for t in OWN:
                 silu(acted[2 + u][:, t, :], mixed[t, 1][:, cols])
             silu(acted[2 + u][:, 2:, :], mixed_late[:, :, cols])
-        middle = CHUNK // RUN // 2
+        middle = CHUNK // WALK // 2
         for c in (2, 3):
             weigh(c, last=middle)
             second_product(c - 1, 2)
@@ -290,7 +291,7 @@ def tile_picked_scoremix_silu_po_kernel(
         for first, last in ((0, HALF), (HALF, S)):
             nc.sync.dma_start(out_words[:, first:last], y_codes[:, first:last])
         for q in range(P // QUADRANT):
-            queue = nc.sync if q % 2 == 0 else nc.scalar
+            queue = nc.scalar if q == 0 else nc.sync
             queue.dma_start(
                 out_2[0].bitcast(I32)[4 * q : 4 * q + 4, :], y_scales[:].bitcast(I32)[QUADRANT * q : QUADRANT * q + 4, :]
             )

from contextlib import ExitStack

import concourse.mybir as mybir

K, T, S, N, G, H = 512, 2048, 512, 512, 2048, 512
FLOPS = 2 * K * H * S + 2 * H * N * S

F32 = mybir.dt.float32
BF16 = mybir.dt.bfloat16
I32 = mybir.dt.int32
U32 = mybir.dt.uint32
U16 = mybir.dt.uint16
U8 = mybir.dt.uint8
FP8X4 = mybir.dt.float8_e4m3fn_x4
FP4X4 = mybir.dt.float4_e2m1fn_x4
ADD = mybir.AluOpType.add
MULT = mybir.AluOpType.mult
COPY = mybir.ActivationFunctionType.Copy
SILU = mybir.ActivationFunctionType.Silu

P = 128
PACK = 4
GROUP = 16
BLOCK_ROWS = 8
QUADRANT = 32
RUN = 4
WALK = 2
HALF = S // 2
HALF_LIST = HALF // GROUP
CHUNK = 128
CHUNKS = S // CHUNK
BANKS = 8
OWN = (0, 1)
FETCHED = (2, 3)
SILU_SCALE = 0.0625 * 0.5


def tile_picked_scoremix_silu_po_kernel(
    tc, x_words, x_scales, d_words, d_scales, gn, w1_words, w1_scales, offs, kidx, nb, out_0, out_1, out_2
):
    nc = tc.nc
    with ExitStack() as ctx:
        lists = ctx.enter_context(tc.tile_pool(name="lists", bufs=1))
        keep = ctx.enter_context(tc.tile_pool(name="keep", bufs=1))
        placed = ctx.enter_context(tc.tile_pool(name="placed", bufs=1))
        held = ctx.enter_context(tc.tile_pool(name="held", bufs=1))
        psum = ctx.enter_context(tc.psum_pool(name="psum", bufs=1))

        kidx_sb = lists.tile([P, H // GROUP], U16, name="kidx_sb")
        offs_sb = lists.tile([P, S // GROUP], U16, name="offs_sb")
        nb_sb = lists.tile([P, S // GROUP], U16, name="nb_sb")

        def sb(name, shape, dtype, slot_of=None):
            return keep.tile(shape, dtype, name=name, tag=slot_of or name, align_bytes=64)

        def place(name, shape, dtype, offset):
            return placed.tile(shape, dtype, name=name, align_bytes=64, offset=offset)

        def list_half(entries, h):
            return entries[:, h * HALF_LIST : (h + 1) * HALF_LIST]

        def deal_bytes(dealt, plain):
            nc.vector.tensor_copy(
                dealt.rearrange("p (t m) -> p t m", t=PACK), plain.rearrange("p (m t) -> p t m", t=PACK)
            )

        d_offset = 4 * T
        d_scale_table = place("d_scale_table", [P, G], U8, d_offset + 4 * G)
        x_scale_table = sb("x_scale_table", [P, T], U8)
        d_table = place("d_table", [P, G], I32, d_offset)
        x_table = place("x_table", [P, T], I32, 0)
        planes = sb("planes", [P, H + S + N], U8)
        w_scale_raw = sb("w_scale_raw", [P, N], U8)
        seed = place("seed", [P, 32], F32, d_offset - 64)
        zero = sb("zero", [P, 1], F32)
        silu_bias = sb("silu_bias", [P, 1], F32)

        nc.vector.memset(w_scale_raw[:].bitcast(I32), 0)
        nc.vector.memset(d_scale_table[:].bitcast(I32), 0)
        nc.vector.memset(seed[:], 0.0)
        nc.vector.memset(x_scale_table[:].bitcast(I32), 0)
        nc.vector.tensor_reduce(zero[:], seed[:], mybir.AxisListType.X, ADD)

        nc.scalar.dma_start(w_scale_raw[:].bitcast(I32)[0:P:BLOCK_ROWS, :], w1_scales[0].bitcast(I32))
        nc.sync.dma_start(kidx_sb[:], kidx)
        nc.sync.dma_start(offs_sb[:], offs)
        nc.sync.dma_start(nb_sb[:], nb)
        nc.sync.dma_start(d_scale_table[:].bitcast(I32)[0:P:BLOCK_ROWS, :], d_scales[0].bitcast(I32))
        nc.sync.dma_start(x_scale_table[:].bitcast(I32)[0:P:BLOCK_ROWS, :], x_scales[0].bitcast(I32))
        nc.sync.dma_start(d_table[:], d_words[0].rearrange("p n t -> p (n t)").bitcast(I32))
        nc.sync.dma_start(x_table[:], x_words[0].rearrange("p n t -> p (n t)").bitcast(I32))
        nc.scalar.activation(silu_bias[:], zero[:], SILU)

        d_plane, x_plane, w_plane = planes[:, :H], planes[:, H : H + S], planes[:, H + S :]
        deal_bytes(w_plane, w_scale_raw[:])
        d_scale_picked = sb("d_scale_picked", [P, H], U8)
        x_scale_picked = sb("x_scale_picked", [P, S], U8)
        nc.vector.tensor_copy(d_scale_picked[:], d_scale_table[:].indirect(kidx_sb[:]))
        nc.vector.tensor_copy(x_scale_picked[:], x_scale_table[:].indirect(offs_sb[:]))
        deal_bytes(d_plane, d_scale_picked[:])
        nc.vector.tensor_copy(x_plane.bitcast(I32), x_scale_picked[:].bitcast(I32))
        for a in range(1, QUADRANT // BLOCK_ROWS):
            nc.scalar.dma_start(
                planes[:].bitcast(I32)[a:P:QUADRANT, :], planes[:].bitcast(I32)[BLOCK_ROWS * a : P : QUADRANT, :]
            )
        w_raw = sb("w_raw", [P, 2 * N], U8, slot_of="x_scale_picked")
        nc.sync.dma_start(w_raw[:].bitcast(I32), w1_words[0].bitcast(I32))

        d_picked = sb("d_picked", [P, H], I32, slot_of="x_scale_table")
        d_dealt = [sb("d_dealt_own", [P, 2, P], I32), place("d_dealt_fetched", [P, 2, P], I32, 0)]
        for h in range(2):
            nc.vector.tensor_copy(
                d_picked[:, h * HALF : (h + 1) * HALF].bitcast(U32),
                d_table[:].bitcast(U32).indirect(list_half(kidx_sb, h)),
            )
        runs = HALF // (PACK * RUN)
        d_plain = d_picked[:].rearrange("p (c i t) -> p c t i", t=PACK, i=RUN)
        for h in range(2):
            nc.vector.tensor_copy(
                d_dealt[0][:].rearrange("p t (c i) -> p c t i", i=RUN)[:, h * runs : (h + 1) * runs],
                d_plain[:, h * runs : (h + 1) * runs, :2],
            )
        gn_sb = place("gn_sb", [P, PACK], F32, d_offset)
        nc.sync.dma_start(gn_sb[:], gn.rearrange("(p t) o -> p (t o)", t=PACK))
        x_picked = [
            sb("x_picked0", [P, HALF], I32),
            sb("x_picked1", [P, HALF], I32, slot_of="d_scale_picked"),
        ]
        for h in range(2):
            nc.vector.tensor_copy(
                x_picked[h][:].bitcast(U32), x_table[:].bitcast(U32).indirect(list_half(offs_sb, h))
            )

        nc.vector.tensor_copy(d_dealt[1][:].rearrange("p t (c i) -> p c t i", i=RUN), d_plain[:, :, 2:])

        window = [sb("window%d" % t, [P, S], F32) for t in range(PACK)]
        passes = [(t, h) for h in range(2) for t in OWN] + [(t, h) for t in FETCHED for h in range(2)]
        for n, (t, h) in enumerate(passes):
            scores = psum.tile([P, HALF], F32, name="s%d%d" % (t, h), tag="bank%d" % n)
            nc.tensor.matmul_mx(
                out=scores[:],
                lhsT=d_dealt[t // 2][:, t % 2, :].bitcast(FP8X4),
                lhsT_scale=d_plane[:, t * P : (t + 1) * P],
                rhs=x_picked[h][:].bitcast(FP8X4),
                rhs_scale=x_plane[:, h * HALF : (h + 1) * HALF],
                start=True,
                stop=True,
            )
            nc.scalar.copy(window[t][:, h * HALF : (h + 1) * HALF], scores[:])

        w_dealt = sb("w_dealt", [P, 2 * N], U8)
        nc.vector.tensor_copy(
            w_dealt[:].bitcast(U16).rearrange("p (t m) -> p t m", t=PACK),
            w_raw[:].bitcast(U16).rearrange("p (m t) -> p t m", t=PACK),
        )

        def hold(name, shape, dtype, offset):
            return held.tile(shape, dtype, name=name, align_bytes=64, offset=offset)

        act_bytes = 4 * PACK * CHUNK
        fetched = {
            (2, 0): hold("fetched20", [P, HALF], F32, 2 * act_bytes - 128),
            (3, 0): sb("fetched30", [P, HALF], F32),
            (2, 1): sb("fetched21", [P, HALF], F32),
        }
        doubled = {(t, h): sb("doubled%d%d" % (t, h), [P, HALF], F32) for t in OWN for h in range(2)}
        mixed_first = sb("mixed_first", [P, PACK, HALF], F32)
        mixed = {(t, 0): mixed_first[:, t, :] for t in range(PACK)}
        mixed[0, 1] = sb("mixed01", [P, HALF], F32)[:]
        mixed_late = sb("mixed_late", [P, 2, HALF], F32)
        mixed[2, 1], mixed[3, 1] = mixed_late[:, 0, :], mixed_late[:, 1, :]

        def double(t, h):
            nc.vector.tensor_scalar(doubled[t, h][:], window[t][:, h * HALF : (h + 1) * HALF], 2.0, None, MULT)

        def mix(t, h):
            nc.vector.tensor_tensor(mixed[t, h], window[t][:].indirect(list_half(nb_sb, h)), doubled[t, h][:], ADD)

        def fetch(t, h):
            nc.scalar.activation(fetched[t, h][:], window[t][:].indirect(list_half(nb_sb, h)), COPY)

        def add_fetched(t, h):
            own = window[t][:, h * HALF : (h + 1) * HALF]
            nc.vector.scalar_tensor_tensor(mixed[t, h], own, 2.0, fetched[t, h][:], MULT, ADD)

        y_scales = sb("y_scales", [P, S], U8)
        y_codes = sb("y_codes", [P, S], I32)
        out_rows = out_0.rearrange("(p t) n -> p t n", t=PACK)
        out_words = out_1[0].rearrange("p n t -> p (n t)").bitcast(I32)
        acted, z, y, y_bf, acc = {}, {}, {}, {}, {}

        def woven(ap):
            return ap.rearrange("p (c i t) -> p c t i", i=WALK, t=PACK)

        def planar(ap):
            return ap.rearrange("p t (c i) -> p c t i", i=WALK)

        def silu(out, in_):
            nc.scalar.activation(out, in_, SILU, bias=silu_bias[:], scale=SILU_SCALE)

        def weigh(c, first=0, last=CHUNK // WALK):
            if first == 0:
                z[c] = sb("z%d" % c, [P, CHUNK * PACK], BF16)
            weights = gn_sb[:].unsqueeze(1).unsqueeze(3).to_broadcast([P, last - first, PACK, WALK])
            nc.vector.tensor_tensor(woven(z[c][:])[:, first:last], planar(acted[c][:])[:, first:last], weights, MULT)

        free_banks = list(range(BANKS)) * 2

        def second_product(c, banks):
            z_codes = sb("z_codes%d" % c, [P, CHUNK], I32)
            z_scales = sb("z_scales%d" % c, [P, CHUNK], U8)
            nc.vector.quantize_mx(out=z_codes[:].bitcast(FP8X4), scales=z_scales[:], in_=z[c][:])
            share = PACK // banks
            acc[c] = []
            for b in range(banks):
                bank = psum.tile([P, share, CHUNK], F32, name="y%d%d" % (c, b), tag="bank%d" % free_banks.pop(0))
                acc[c].append(bank)
                for u in range(share):
                    t = share * b + u
                    nc.tensor.matmul_mx(
                        out=bank[:, u, :],
                        lhsT=w_dealt[:, 2 * t * P : 2 * (t + 1) * P].bitcast(FP4X4),
                        lhsT_scale=w_plane[:, t * P : (t + 1) * P],
                        rhs=z_codes[:].bitcast(FP8X4),
                        rhs_scale=z_scales[:],
                        start=True,
                        stop=True,
                    )

        def empty(c):
            y[c] = sb("y%d" % c, [P, PACK, CHUNK], F32)
            share = PACK // len(acc[c])
            for b, bank in enumerate(acc[c]):
                nc.scalar.copy(y[c][:, share * b : share * (b + 1), :], bank[:])
            nc.sync.dma_start(out_rows[:, :, c * CHUNK : (c + 1) * CHUNK], y[c][:])

        def round_result(c, slot_of=None):
            y_bf[c] = sb("y_bf%d" % c, [P, CHUNK * PACK], BF16, slot_of)
            nc.vector.tensor_copy(woven(y_bf[c][:]), planar(y[c][:]))

        def quantise_result(c):
            cols = slice(c * CHUNK, (c + 1) * CHUNK)
            nc.vector.quantize_mx(out=y_codes[:, cols].bitcast(FP8X4), scales=y_scales[:, cols], in_=y_bf[c][:])

        double(0, 0)
        double(1, 0)
        double(0, 1)
        mix(0, 0)
        double(1, 1)
        mix(1, 0)
        mix(0, 1)
        fetch(2, 0)
        fetch(3, 0)
        add_fetched(2, 0)
        add_fetched(3, 0)
        mixed[1, 1] = hold("mixed11", [P, HALF], F32, 2 * act_bytes)[:]
        mix(1, 1)
        fetch(2, 1)
        add_fetched(2, 1)
        acted[0] = hold("acted0", [P, PACK, CHUNK], F32, act_bytes - 64)
        silu(acted[0][:, :2, :], mixed_first[:, :2, :CHUNK])
        silu(acted[0][:, 2:, :], mixed_first[:, 2:, :CHUNK])
        fetched[3, 1] = sb("fetched31", [P, HALF], F32, "fetched30")
        fetch(3, 1)
        weigh(0)
        add_fetched(3, 1)
        second_product(0, 1)
        acted[1] = sb("acted1", [P, PACK, CHUNK], F32)
        silu(acted[1][:], mixed_first[:, :, CHUNK:])
        weigh(1)
        for u in range(2):
            cols = slice(u * CHUNK, (u + 1) * CHUNK)
            acted[2 + u] = hold("acted%d" % (2 + u), [P, PACK, CHUNK], F32, u * act_bytes)
            for t in OWN:
                silu(acted[2 + u][:, t, :], mixed[t, 1][:, cols])
            silu(acted[2 + u][:, 2:, :], mixed_late[:, :, cols])
        middle = CHUNK // WALK // 2
        for c in (2, 3):
            weigh(c, last=middle)
            second_product(c - 1, 2)
            weigh(c, first=middle)
        empty(0)
        round_result(0)
        second_product(3, PACK)
        for c in range(1, CHUNKS):
            empty(c)
            round_result(c, slot_of="z_codes3" if c == 2 else None)
            quantise_result(c - 1)
        quantise_result(CHUNKS - 1)

        for first, last in ((0, HALF), (HALF, S)):
            nc.sync.dma_start(out_words[:, first:last], y_codes[:, first:last])
        for q in range(P // QUADRANT):
            queue = nc.scalar if q == 0 else nc.sync
            queue.dma_start(
                out_2[0].bitcast(I32)[4 * q : 4 * q + 4, :], y_scales[:].bitcast(I32)[QUADRANT * q : QUADRANT * q + 4, :]
            )
